import numpy as np, ml_dtypes
CORES = [48,51,52,55]
N = 4
BF = ml_dtypes.bfloat16
def gentries(a):
    return np.ascontiguousarray(a.reshape(8, 16, -1).transpose(0, 2, 1)).reshape(8, -1)
def gtable(e):
    e = np.asarray(e); return np.ascontiguousarray(e.reshape(8, -1, 16).transpose(0, 2, 1)).reshape(128, -1).astype(np.int32)
W, UM, O, T, ST = 4096, 4096, 256, 5, 1
def parts(rng):
    x = rng.integers(0, 256, (N, 128, W), dtype=np.int16)
    p = rng.integers(0, W, (N, 8, W)); v = rng.integers(0, W, (N, 8, O, 16)); y = rng.integers(0, 256, (N, 128, O)); w = rng.integers(0, 256, (N, 128, 1))
    lm = np.zeros((N, 8, 2), np.int64)
    for q in range(N):
        lm[q, :, 0] = rng.permutation(np.array([400, 1000, 1150, 1300, 1400, 1550, 1700, 2600])) + rng.integers(-50, 51, 8)
        lm[q, :, 1] = rng.permutation(np.array([1100, 1200, 1300, 1400, 1500, 1600, 1700, 1800])) + rng.integers(-50, 51, 8)
    return x, p, v, y, w, lm
def pack(x, p, v, y, w, lm):
    return {"claim": np.ascontiguousarray(x).astype(np.float32).astype(BF), "par": np.ascontiguousarray(p).astype(np.int32), "who": np.stack([gtable(a.reshape(8, -1)) for a in v]),
            "est": np.ascontiguousarray(y).astype(np.float32).astype(BF), "wt": np.ascontiguousarray(w).astype(np.int32), "lim": np.ascontiguousarray(lm).astype(np.int32)}
def setup_inputs(rng):
    return pack(*parts(rng))
def setup_inputs_spread(rng):
    x, p, v, y, w, lm = parts(rng)
    x = (x.reshape(N, 8, 16, W) >> rng.integers(0, 9, (N, 8, 1, W)).astype(np.int16)).reshape(N, 128, W)
    p = np.minimum((W * rng.random(p.shape) ** 2).astype(np.int64), W - 1); v = np.minimum((W * rng.random(v.shape) ** 3).astype(np.int64), W - 1)
    y = (y.reshape(N, 8, 16, O) >> rng.integers(0, 9, (N, 8, 1, O))).reshape(N, 128, O); w = w >> rng.integers(0, 8, w.shape)
    lm = np.minimum(np.exp2(5 + 7 * rng.random(lm.shape)).astype(np.int64), 4080)
    return pack(x, p, v, y, w, lm)
def setup_inputs_ends(rng):
    c = rng.integers(0, 4, (N, 8, 1, W), dtype=np.int16); x = (255 * np.where(c < 2, c, rng.integers(0, 2, (N, 8, 16, W), dtype=np.int16))).reshape(N, 128, W)
    p = (W - 1) * rng.integers(0, 2, (N, 8, W))
    v = np.where(rng.random((N, 8, O, 1)) < 0.2, rng.integers(0, W, (N, 8, O, 16)), (W - 1) * rng.integers(0, 2, (N, 8, O, 16)))
    c = rng.integers(0, 4, (N, 8, 1, O)); y = (255 * np.where(c < 2, c, rng.integers(0, 2, (N, 8, 16, O)))).reshape(N, 128, O)
    w = 255 * rng.integers(0, 2, (N, 8, 16)); w[:, 3] = 0; w[:, 7] = 255; w = w.reshape(N, 128, 1)
    lm = np.full((N, 8, 2), 4080, np.int64)
    for q in range(N):
        for b in range(2): lm[q, :7, b] = 4080 * rng.permutation(np.array([0, 0, 0, 0, 1, 1, 1]))
    u = (16 * 255 * 255) & (UM - 1); hl = ((((W - 1) * u) >> 5) + W - 1) & (W - 1); h1 = ((u >> 5) + 1) & (W - 1)
    x[:, 112:, 0] = 0; x[:, 112:, hl] = 255; x[:, 112:, h1] = 255
    p[:, 7, 0] = W - 1; p[:, 7, 1] = 0; p[:, 7, W - 1] = 0
    y[:, 112:, O - 1] = 255; y[:, 112:, 3] = 255
    v[:, 7, O - 1] = 0; v[:, 7, O - 1, 14] = W - 1; v[:, 7, O - 1, 15] = 1
    v[:, 7, 3] = 0; v[:, 7, 3, 1] = W - 1; v[:, 7, 3, 2] = W - 1
    return pack(x, p, v, y, w, lm)
def setup_inputs_corners(rng):
    x, p, v, y, w, lm = parts(rng); sh = int(rng.integers(0, 8)); a = np.arange(W)
    for q in range(N):
        for g in range(8):
            m = (g + q + sh) % 8; lo, hi = 16 * g, 16 * g + 16
            if m == 0:
                p[q, g] = np.minimum(a + 1, W - 1); lm[q, g] = (4080, 1500); v[q, g, 0] = W - 1; v[q, g, 1] = 0; v[q, g, O - 1, 15] = W - 2
            elif m == 1:
                p[q, g] = a; lm[q, g] = (1, 0)
            elif m == 2:
                p[q, g] = 0; lm[q, g] = (0, 0); v[q, g] = rng.integers(0, W, (O, 1)); v[q, g, ::2] = W - 1
            elif m == 3:
                pool = np.concatenate([np.array([0, W - 1]), 1 + rng.permutation(W - 2)[:6]]); v[q, g] = pool[rng.integers(0, 8, (O, 16))]; p[q, g] = W - 1; lm[q, g] = (1300, 0)
            elif m == 4:
                w[q, lo:hi] = 0; lm[q, g] = (1, 0)
                e = rng.permutation(W)[:19]; c = x[q, lo:hi]
                c[:, e[:16]] = 255; c[np.arange(14), e[1:15]] = 0; c[14:, e[15]] = 0
                c[:, e[16:18]] = 0; c[:, e[18]] = 127
                p[q, g, e[:16]] = e[16]; p[q, g, e[16:18]] = e[1]; p[q, g, e[18]] = e[18]
                v[q, g, O - 1] = e[:16]
                v[q, g, O - 2] = e[:16]; v[q, g, O - 2, 0] = e[18]
                v[q, g, 0] = e[16]; v[q, g, 0, 0] = e[0]; v[q, g, O - 3] = e[17]; v[q, g, O - 3, 0] = e[0]
            elif m == 5:
                w[q, lo:hi] = 255; y[q, lo:hi] = 255; lm[q, g] = (1300, 4080)
            elif m == 6:
                v[q, g] = rng.permutation(W)[:16 * O].reshape(O, 16); lm[q, g] = (1200, 0)
            else:
                p[q, g] = W - 1 - a; w[q, lo:hi] = 0; w[q, lo + int(rng.integers(0, 16))] = 1; y[q, lo:hi, 0] = 0; lm[q, g] = (4080, 0)
    return pack(x, p, v, y, w, lm)
def setup_inputs_counts(rng):
    x, p, v, y, w, lm = parts(rng); a = int(rng.integers(0, N)); b = (a - ST) % N; d = (a - 2 * ST) % N; s = np.arange(W)
    p[d, :, :64] = np.arange(64); v[d] = rng.integers(0, 63, (8, O, 16)); lm[d, :, 0] = 1360 + rng.integers(-50, 51, 8)
    lm[b, :, 0] = 0; v[b] = rng.integers(64, W, (8, O, 16))
    w[a] = 0; x[a] = (x[a] & 63) + 191 * (s & 1)
    p[a] = (p[a] - (p[a] & 1)) + ((s + (s >= 64)) & 1); p[a, :, 63] = 63
    lm[a, :, 0] = 340 + rng.integers(-20, 21, 8); lm[a, :, 1] = 4080
    v[a] = rng.integers(64, W, (8, O, 16)); v[a, 7, O - 1] = 63; v[a, 0, 0, :15] = 63
    return pack(x, p, v, y, w, lm)
def setup_inputs_ties(rng):
    x, p, v, y, w, lm = parts(rng)
    z = np.stack([rng.permutation(np.array([1, 1, 3, 3, 8, 31, 64, 85])) for q in range(N)])
    x = ((x & 3).reshape(N, 8, 16, W) * z[:, :, None, None]).reshape(N, 128, W)
    lm = np.stack([z * rng.integers(17, 23, (N, 8)), z * rng.integers(18, 27, (N, 8))], axis=2)
    v[:, ::3] = v[:, ::3] & 63
    return pack(x, p, v, y, w, lm)
def check_inputs(d):
    bad = []
    for k, lo, hi in (("claim", 0, 255), ("par", 0, W - 1), ("who", 0, W - 1), ("est", 0, 255), ("wt", 0, 255), ("lim", 0, 4080)):
        a = np.asarray(d[k]).astype(np.float32)
        if not (np.min(a) >= lo and np.max(a) <= hi): bad.append("range of " + k)
        elif not np.all(np.floor(a) == a): bad.append("whole numbers of " + k)
    return bad
def place(s, u, t):
    return (((s * u[:, :, None]) >> 5) + s + 77 * t) & (W - 1)
def reference(claim, par, who, est, wt, lim):
    X = np.ascontiguousarray(np.asarray(claim).astype(np.float32).astype(np.int32).reshape(N, 8, 16, W).transpose(0, 1, 3, 2))
    P = np.asarray(par).astype(np.int64); V = np.stack([gentries(a) for a in who]).astype(np.int64).reshape(N, 8, O, 16)
    Y = np.ascontiguousarray(np.asarray(est).astype(np.float32).astype(np.int64).reshape(N, 8, 16, O).transpose(0, 1, 3, 2))
    wq = np.asarray(wt).astype(np.int64).reshape(N, 8, 1, 16); lm = np.asarray(lim).astype(np.int64)
    G = np.arange(8)[:, None]; cnt = [0] * N
    for t in range(T):
        for q in range(N):
            r = (q - ST * t) % N; v = V[r]; y0 = Y[r]
            u = np.add.reduce(wq[q] * y0, axis=2) & (UM - 1)
            p = P[q][G, v.reshape(8, -1)].reshape(8, O, 16)
            x = X[q][G, place(v, u, t).reshape(8, -1)].reshape(8, O, 16, 16)
            z = X[q][G, place(p, u, t).reshape(8, -1)].reshape(8, O, 16, 16)
            dep = np.add.reduce(np.abs(x - z), axis=3) < lm[q, :, 0][:, None, None] + cnt[q]
            cand = ~dep | np.all(dep, axis=2, keepdims=True)
            M = (np.max(np.where(cand[..., None], x, -1), axis=2) + np.min(np.where(cand[..., None], x, 256), axis=2)) >> 1
            far = np.where(cand, np.add.reduce(np.abs(x - M[:, :, None, :]), axis=3), 1 << 20)
            y = np.take_along_axis(x, np.argmin(far, axis=2)[:, :, None, None], 2)[:, :, 0, :]
            err = np.add.reduce(np.abs(x - y[:, :, None, :]), axis=3)
            j = np.argmax(err, axis=2)[:, :, None]; rest = np.where(np.arange(16) == j, -1, err); k = np.argmax(rest, axis=2)[:, :, None]
            ask = np.take_along_axis(rest, k, 2)[:, :, 0] >= lm[q, :, 1][:, None]
            vj = np.take_along_axis(v, j, 2)[:, :, 0]; vk = np.take_along_axis(v, k, 2)[:, :, 0]
            for g in range(8):
                o = np.nonzero(ask[g])[0]
                if len(o):
                    s, first = np.unique(vk[g, o], return_index=True)
                    P[q, g, s] = vj[g, o[first]]
            V[r] = np.where(dep, p, v); Y[r] = (y0 + y) >> 1
            cnt[q] = int(np.count_nonzero(dep)) & 31
    return {"yv": np.stack([gtable(a.reshape(8, -1)) for a in V]).astype(np.float32), "ye": np.ascontiguousarray(Y.transpose(0, 1, 3, 2)).reshape(N, 128, O).astype(np.float32).astype(BF), "yp": P.astype(np.float32)}

@@ -1,0 +1,673 @@
+import numpy as np
+from concourse.mybir import AluOpType, AxisListType, ActivationFunctionType
+
+A = AluOpType
+AF = ActivationFunctionType
+VIS = 5
+BLOCKS = [(0, 64), (64, 128), (128, 192), (192, 256)]
+BUF = {}
+SEMAPHORES = ["vv", "ss", "pp", "gg"]
+
+
+def _b(name, shape, dtype="float32", where="sbuf"):
+    BUF[name] = (where, shape, dtype)
+
+
+BF, F32, I32, U16 = "bfloat16", "float32", "int32", "uint16"
+_b("claimw", [128, 4096], BF)
+_b("parw", [128, 4368], BF)
+for _t in range(VIS):
+    _b("yb%d" % _t, [128, 256], BF)
+    _b("vb%d" % _t, [128, 256], F32)
+    _b("yn%d" % _t, [128, 256], BF)
+    _b("vn%d" % _t, [128, 256], F32)
+    _b("thc%d" % _t, [128, 8], F32)
+for _n in ("x0", "x1", "xs", "pr", "d", "ad", "af", "ae", "mx", "mn"):
+    _b(_n, [128, 4096], BF)
+for _n in ("um0", "um1", "hi0", "hi1", "t1", "t2", "t3", "msum", "mhalf", "yhalf", "aint"):
+    _b(_n, [128, 256], I32)
+for _n in ("hl", "zl", "vl", "h2l"):
+    _b(_n, [128, 256], U16)
+for _n in ("q1", "q2", "dif", "vm", "fh", "dlt", "h2f", "sa", "sb", "cr", "dg", "cs", "tt_"):
+    _b(_n, [128, 256], F32)
+for _n in ("dep", "mm_", "yy", "ohb", "adat", "oc"):
+    _b(_n, [128, 256], BF)
+_b("tr", [128, 512], F32)
+_b("kint", [128, 64], I32)
+_b("yl", [128, 16], U16)
+_b("pm", [128, 512], F32)
+_b("code", [128, 64], I32)
+_b("ask", [128, 32], F32)
+_b("kk", [128, 32], BF)
+_b("ktb", [16, 256], BF)
+_b("bia", [128, 16], F32)
+_b("sint", [128, 32], I32)
+_b("dd", [128, 4096], F32)
+_b("dmin", [128, 16], F32)
+_b("dfl", [128, 64], F32)
+_b("ol", [128, 16], U16)
+_b("dsum", [128, 2], F32)
+_b("cint", [128, 2], I32)
+for _n in ("ones", "eye", "neye", "blk", "blk1", "blk8k", "tri", "trim", "dm32", "wmat", "j1", "j2", "kt", "r2"):
+    _b(_n, [128, 128], BF)
+for _n in ("sx", "px", "r1", "rm"):
+    _b(_n, [128, 2048], BF)
+for _n in ("blkf", "blk512", "onesf", "dmask"):
+    _b(_n, [128, 128], F32)
+_b("exs", [16, 512], BF)
+_b("exf", [16, 128], F32)
+_b("eyef", [16, 16], F32)
+_b("io1", [128, 128], I32)
+_b("io2", [128, 128], I32)
+_b("pcol", [128, 4], I32)
+_b("cols", [128, 16], F32)
+_b("wti", [128, 1], I32)
+_b("wtf", [128, 1], F32)
+_b("limi", [8, 2], I32)
+_b("limf", [8, 2], F32)
+_b("limd", [8, 8], F32)
+_b("tht", [128, 16], F32)
+_b("thb", [128, 2], F32)
+_b("dcon", [128, 16], F32)
+_b("iod", [128, 16], I32)
+_b("whoi", [128, 256], I32)
+_b("pari", [128, 256], I32)
+_b("parlh", [128, 512], I32)
+_b("parb", [128, 512], BF)
+_b("ypf", [128, 256], F32)
+_b("dlo", [8, 4096], BF, "dram")
+_b("dhi", [8, 4096], BF, "dram")
+for _n in ("pz0", "pz1", "pu", "pk", "pa", "pf0", "pf1", "pf2"):
+    _b(_n, [128, 512], F32, "psum")
+
+for _n in ("who", "est", "wt", "lim", "par", "claim0", "claim1", "plo", "phi", "pwin", "yv0", "yv1", "ye0", "ye1", "yp"):
+    SEMAPHORES.append("l_" + _n)
+for _t in range(1, VIS):
+    for _h in range(2):
+        for _k in "yv":
+            SEMAPHORES += ["a%s%d%d" % (_k, _t, _h), "o%s%d%d" % (_k, _t, _h)]
+
+PACK = {}
+SCRATCH = {}
+_ROOM = {}
+_KEEP = ("claimw", "parw", "whoi", "pari", "parb", "ypf", "wti", "limi", "hl", "zl", "vl", "h2l", "yl", "ol", "dd", "adat")
+for _n, (_w, _sh, _d) in BUF.items():
+    if _w == "sbuf" and _n not in _KEEP and _n[:2] not in ("yb", "vb", "yn", "vn") and _sh[0] == 128 and _sh[1] <= 512:
+        PACK[_n] = ("pack_" + _d, _ROOM.get(_d, 0))
+        _ROOM[_d] = _ROOM.get(_d, 0) + (_sh[1] + 15) // 16 * 16
+    else:
+        SCRATCH[_n] = BUF[_n]
+for _d in _ROOM:
+    SCRATCH["pack_" + _d] = ("sbuf", [128, _ROOM[_d]], _d)
+
+_CACHE = {}
+CY, PCY, GATH, SCAT = 0.001, 0.0006, 1.55, 3.5
+VOV, SOV, POV, LAT = 0.03, 0.04, 0.03, 0.1
+SEED, EPS = 0, 0.0
+XL = 64
+
+
+def S(name, a, b, step=1, p=128):
+    return (name, a, b, step, p)
+
+
+def IND(name, a, b, off, c, d):
+    return (name, a, b, off, c, d, "ind")
+
+
+def ap(T, s):
+    if s[0] in PACK:
+        r, o = PACK[s[0]]
+        return T[r][0:s[4], o + s[1]:o + s[2]] if s[3] == 1 else T[r][0:s[4], o + s[1]:o + s[2]:s[3]]
+    if len(s) == 7:
+        return T[s[0]][:, s[1]:s[2]].indirect(T[s[3]][:, s[4]:s[5]])
+    t = T[s[0]]
+    if s[3] == 1:
+        return t[0:s[4], s[1]:s[2]]
+    return t[0:s[4], s[1]:s[2]:s[3]]
+
+
+def regs(s):
+    if len(s) == 7:
+        return [(s[0], s[1], s[2]), (s[3], s[4], s[5])]
+    return [(s[0], s[1], s[2])]
+
+
+def width(s):
+    if len(s) == 7:
+        return 16 * (s[5] - s[4])
+    return (s[2] - s[1] + s[3] - 1) // s[3]
+
+
+def half(*ss):
+    return all(BUF[s[0]][2] in (BF, U16) for s in ss)
+
+
+def build(nE):
+    ops = []
+
+    def add(q, fns, R, W, cost, sem=None, val=0, send=None):
+        rr = [r for s in R for r in regs(s)]
+        ww = [(s[0], s[1], s[2]) for s in W]
+        offs = [(s[3], s[4], s[5]) for s in W if len(s) == 7]
+        ops.append({"q": q, "f": fns, "R": rr + offs, "W": ww, "c": cost, "sem": sem, "val": val, "send": send})
+        return len(ops) - 1
+
+    def vcost(n, f=1.0):
+        return max(64, n * f) * CY + VOV
+
+    def tt(out, a, b, op):
+        n = width(b)
+        if len(a) == 7:
+            f = GATH
+        else:
+            f = 1.0 if "psum" in (BUF[a[0]][0], BUF[b[0]][0]) else 2.0
+        add("V", [lambda g, T: g.vector.tensor_tensor(out=ap(T, out), in0=ap(T, a), in1=ap(T, b), op=op)], [a, b], [out], vcost(n, f))
+
+    def cp(out, a):
+        f = SCAT if len(out) == 7 else GATH if len(a) == 7 else 0.5 if half(out, a) else 1.0
+        add("V", [lambda g, T: g.vector.tensor_copy(out=ap(T, out), in_=ap(T, a))], [a], [out], vcost(width(a), f))
+
+    def ts(out, a, s1, op0, s2=None, op1=None):
+        R = [a] + [s for s in (s1, s2) if isinstance(s, tuple)]
+
+        def f(g, T):
+            x1 = ap(T, s1) if isinstance(s1, tuple) else s1
+            x2 = ap(T, s2) if isinstance(s2, tuple) else s2
+            if op1 is None:
+                return g.vector.tensor_scalar(out=ap(T, out), in0=ap(T, a), scalar1=x1, scalar2=None, op0=op0)
+            return g.vector.tensor_scalar(out=ap(T, out), in0=ap(T, a), scalar1=x1, scalar2=x2, op0=op0, op1=op1)
+        add("V", [f], R, [out], vcost(width(a), 0.5 if half(out, a) else 1.0))
+
+    def scan(out, d0, d1, init, op0, op1):
+        add("V", [lambda g, T: g.vector.tensor_tensor_scan(out=ap(T, out), data0=ap(T, d0), data1=ap(T, d1), initial=init, op0=op0, op1=op1)],
+            [d0, d1], [out], vcost(width(d1), 0.5 if half(out, d0, d1) else 1.0))
+
+    def red(out, a, op, absv=False):
+        if absv:
+            fn = lambda g, T: g.vector.tensor_reduce(out=ap(T, out), in_=ap(T, a), axis=AxisListType.X, op=op, apply_absolute_value=True)
+        else:
+            fn = lambda g, T: g.vector.tensor_reduce(out=ap(T, out), in_=ap(T, a), axis=AxisListType.X, op=op)
+        add("V", [fn], [a], [out], vcost(width(a)))
+
+    def fill(out, c):
+        add("V", [lambda g, T: g.vector.memset(ap(T, out), c)], [], [out], vcost(width(out)))
+
+    def act(out, a, func, bias=None, scale=None):
+        R = [a] + ([bias] if isinstance(bias, tuple) else [])
+
+        def f(g, T):
+            kw = {}
+            if bias is not None:
+                kw["bias"] = ap(T, bias) if isinstance(bias, tuple) else bias
+            if scale is not None:
+                kw["scale"] = scale
+            return g.scalar.activation(out=ap(T, out), in_=ap(T, a), func=func, **kw)
+        add("S", [f], R, [out], max(64, width(a) * (GATH if len(a) == 7 else 1.0)) * CY + SOV)
+
+    def mm(groups):
+        fns = []
+        c = POV
+        for (o, l, r, st, sp) in groups:
+            fns.append(lambda g, T, o=o, l=l, r=r, st=st, sp=sp: g.tensor.matmul(out=ap(T, o), lhsT=ap(T, l), rhs=ap(T, r), start=st, stop=sp))
+            c += max(64, width(r)) * PCY * (4 if BUF[r[0]][2] == F32 else 1)
+        add("P", fns, [r for (o, l, r2, st, sp) in groups for r in (l, r2)], [x[0] for x in groups], c)
+
+    def one(out, l, r):
+        mm([(out, l, r, True, True)])
+
+    def dma(q, sem, pairs, R, W, cost):
+        add(q, [lambda g, T, o=o, i=i: (g.sync if q == "Y" else g.scalar).dma_start(o(T), i(T)) for (o, i) in pairs], R, W, cost, sem=sem, val=16 * len(pairs))
+
+    def iota(out, pattern, base, cm):
+        kw = {"allow_small_or_imprecise_dtypes": True} if BUF[out[0]][2] in (BF, F32) else {}
+        add("G", [lambda g, T: g.iota(ap(T, out), pattern, base, cm, **kw)], [], [out], 0.13 + 2 * width(out) * CY)
+
+    def asel(out, a, pattern, op, base, cm):
+        add("G", [lambda g, T: g.affine_select(ap(T, out), ap(T, a), pattern, op, 0.0, base, cm)], [a], [out], 0.17 + 2 * width(out) * CY)
+
+    def full(name):
+        sh = BUF[name][1]
+        return S(name, 0, sh[1], 1, sh[0])
+
+    dma("Y", "l_who", [(lambda T: T.whoi[:], lambda T: T.who[:])], [], [full("whoi")], 2.0)
+    dma("Y", "l_est", [(lambda T: T.yb0[:], lambda T: T.est[:])], [], [full("yb0")], 2.0)
+    dma("Y", "l_wt", [(lambda T: T.wti[:], lambda T: T.wt[:])], [], [full("wti")], 2.0)
+    dma("S", "l_claim0", [(lambda T: T.claimw[:, 0:2048], lambda T: T.claim[:, 0:2048])], [], [S("claimw", 0, 2048)], 3.0)
+    dma("S", "l_claim1", [(lambda T: T.claimw[:, 2048:4096], lambda T: T.claim[:, 2048:4096])], [], [S("claimw", 2048, 4096)], 4.0)
+    dma("Y", "l_par", [(lambda T: T.pari[:], lambda T: T.par[:])], [], [full("pari")], 2.0)
+    dma("Y", "l_lim", [(lambda T: T.limi[:], lambda T: T.lim[:])], [], [full("limi")], 2.0)
+    fill(full("ones"), 1.0)
+    asel(full("blk1"), full("ones"), [[-16, 8], [0, 16]], A.is_ge, 0, 1)
+    asel(full("blk"), full("blk1"), [[16, 8], [0, 16]], A.is_ge, 15, -1)
+    asel(full("eye"), full("ones"), [[-1, 128]], A.is_equal, 0, 1)
+    iota(S("pcol", 0, 1), [[0, 1]], 0, 1)
+    cp(full("vb0"), full("whoi"))
+    cp(full("vl"), full("vb0"))
+    ts(S("parlh", 0, 256), full("pari"), 255, A.bitwise_and)
+    ts(S("parlh", 256, 512), full("pari"), 8, A.logical_shift_right)
+    cp(full("parb"), full("parlh"))
+    dma("Y", "l_plo", [(lambda T: T.dlo[:], lambda T: T.parb[:, 0:256])], [S("parb", 0, 256)], [S("dlo", 0, 4096, 1, 8)], 2.0)
+    dma("Y", "l_phi", [(lambda T: T.dhi[:], lambda T: T.parb[:, 256:512])], [S("parb", 256, 512)], [S("dhi", 0, 4096, 1, 8)], 2.0)
+    dma("Y", "l_pwin", [(lambda T, i=i: T.parw[i::16, 16:4112], lambda T, i=i: (T.dhi if i % 2 else T.dlo)[:]) for i in range(16)],
+        [S("dlo", 0, 4096, 1, 8), S("dhi", 0, 4096, 1, 8)], [S("parw", 16, 4112)], 8.0)
+    cp(full("wtf"), full("wti"))
+    ts(full("wmat"), full("blk"), S("wtf", 0, 1), A.mult)
+    ts(S("pcol", 1, 2), S("pcol", 0, 1), 15, A.bitwise_and)
+    ts(S("pcol", 2, 3), S("pcol", 0, 1), 1, A.bitwise_and)
+    K16 = S("cols", 0, 1)
+    CODE = S("cols", 1, 2)
+    COLW = S("cols", 2, 3)
+    COLA = S("cols", 3, 4)
+    ACS = S("cols", 7, 8)
+    ACB = S("cols", 8, 9)
+    cp(K16, S("pcol", 1, 2))
+    ts(CODE, K16, -1.0, A.mult, 16.0, A.add)
+    ts(S("cols", 4, 5), K16, 1.0, A.is_equal, 256.0, A.mult)
+    ts(S("cols", 5, 6), K16, 0.0, A.is_equal)
+    tt(COLW, S("cols", 4, 5), S("cols", 5, 6), A.add)
+    ts(COLA, K16, 16.0, A.mult)
+    cp(S("cols", 6, 7), S("pcol", 2, 3))
+    ts(ACS, S("cols", 6, 7), -255.0 / 256.0, A.mult, 1.0, A.add)
+    ts(ACB, S("cols", 6, 7), -0.498, A.mult)
+    fill(full("sx"), 0.0)
+    for k in range(16):
+        cp(S("sx", 129 * k, 128 * k + 128, 16), S("blk", 0, 128, 16))
+    ts(full("px"), full("sx"), COLW, A.mult)
+    ts(full("neye"), full("eye"), -1.0, A.mult)
+    asel(full("tri"), full("blk"), [[1, 128]], A.is_gt, 0, -1)
+    ts(full("trim"), full("eye"), -32.0, A.mult)
+    tt(full("trim"), full("trim"), full("tri"), A.add)
+    ts(full("dm32"), full("eye"), 32.0, A.mult)
+    tt(full("dm32"), full("dm32"), full("blk"), A.subtract)
+    asel(S("exs", 0, 128, 1, 16), S("ones", 0, 128, 1, 16), [[1, 128]], A.is_ge, 0, -16)
+    asel(S("exs", 128, 256, 1, 16), S("exs", 0, 128, 1, 16), [[-1, 128]], A.is_ge, 15, 16)
+    asel(S("exs", 256, 384, 1, 16), S("ones", 0, 128, 1, 16), [[1, 128]], A.is_ge, 128, -16)
+    asel(S("exs", 384, 512, 1, 16), S("exs", 256, 384, 1, 16), [[-1, 128]], A.is_ge, -113, 16)
+    cp(full("exf"), S("exs", 128, 256, 1, 16))
+    cp(full("limf"), full("limi"))
+    cp(full("onesf"), full("ones"))
+    cp(full("eyef"), S("eye", 0, 16, 1, 16))
+    ts(full("limd"), S("eyef", 0, 8, 1, 8), S("limf", 1, 2, 1, 8), A.mult, 32.0, A.mult)
+    mm([(S("pa", 0, 2), S("exf", 0, 128, 1, 8), full("limf"), True, True),
+        (S("pa", 8, 16), S("onesf", 0, 128, 1, 8), full("limd"), True, True)])
+    cp(full("thb"), S("pa", 0, 2))
+    cp(S("thc0", 0, 1), S("pa", 0, 1))
+    fill(S("tht", 0, 8), -1.0)
+    cp(S("tht", 8, 16), S("pa", 8, 16))
+    cp(full("blkf"), full("blk"))
+    fill(full("r1"), 1.0)
+    ts(S("r1", 0, 2048, 16), S("r1", 0, 2048, 16), 0.0, A.mult)
+    fill(full("rm"), 0.0)
+    ts(S("rm", 0, 2048, 16), S("rm", 0, 2048, 16), 256.0, A.add)
+    iota(full("io1"), [[0, 16], [256, 8]], 0, 0)
+    ts(full("j1"), full("io1"), COLA, A.add)
+    iota(full("j2"), [[1, 16], [0, 8]], 0, 0)
+    iota(full("kt"), [[0, 8], [-1, 16]], 16, 0)
+    iota(full("oc"), [[1, 256]], 0, 0)
+    fill(full("r2"), 1.0)
+    ts(S("r2", 1, 128, 16), S("r2", 1, 128, 16), 0.0, A.mult)
+    iota(full("io2"), [[1, 128]], 128, -1)
+    ts(full("io2"), full("io2"), 15, A.bitwise_and)
+    ts(full("dmask"), full("io2"), 0.0, A.is_equal)
+    ts(full("blk512"), full("blk"), 512.0, A.mult)
+    ts(full("blk8k"), full("blk"), 8192.0, A.mult)
+    iota(full("iod"), [[16, 16]], 4112, 0)
+    ts(full("dcon"), full("iod"), K16, A.add)
+    turn = [0]
+
+    def bank():
+        turn[0] += 1
+        return "pf%d" % (turn[0] % 3)
+
+    def send(what, t, h):
+        c = (128 * h, 128 * h + 128)
+        key = "%s%d%d" % (what, t + 1, h)
+        i = add("G", None, [S("%sn%d" % (what, t), *c)], [], 1.0, sem="o" + key, val=nE, send=(what, t + 1, h))
+        add("N", None, [], [S("%sb%d" % (what, t + 1), *c)], 2.0, sem="a" + key, val=nE, send=i)
+
+    def st_names(t, h):
+        c = (128 * h, 128 * h + 128)
+        v = S("vb%d" % t, *c)
+        if t > 0:
+            cp(S("vl", *c), v)
+        act(S("q1", *c), v, AF.Identity, float(2464 * t - 131072), 32.0)
+
+    def st_hash(t, h):
+        c = (128 * h, 128 * h + 128)
+        um, hi = S("um%d" % (t % 2), *c), S("hi%d" % (t % 2), *c)
+        U, W = S("pu", 256 * h, 256 * h + 128), S("pu", 256 * h + 128, 256 * h + 256)
+        one(U, full("wmat"), S("yb%d" % t, *c))
+        cp(S("t1", *c), U)
+        ts(um, S("t1", *c), 4095, A.bitwise_and)
+        tt(W, S("vb%d" % t, *c), um, A.mult)
+        tt(S("t2", *c), W, S("q1", *c), A.add)
+        ts(hi, S("t2", *c), 5, A.arith_shift_right, 4095, A.bitwise_and)
+        cp(S("hl", *c), hi)
+
+    def st_xgather(t, h):
+        c = (128 * h, 128 * h + 128)
+        for a in range(c[0], c[1], XL):
+            act(S("x%d" % (t % 2), 16 * a, 16 * (a + XL)), IND("claimw", 0, 4096, "hl", a, a + XL), AF.Copy)
+
+    def st_pgather(t, n):
+        c = BLOCKS[n]
+        act(S("pr", 16 * c[0], 16 * c[1]), IND("parw", 16, 4112, "vl", *c), AF.Copy)
+
+    def st_z(t, n):
+        c = BLOCKS[n]
+        L = c[1] - c[0]
+        X, X2 = 16 * c[0], 16 * c[1]
+        b = "pz%d" % (n % 2)
+        p, w2, w3, w4 = [S(b, 128 * e, 128 * e + L) for e in range(4)]
+        um, hi, dep = S("um%d" % (t % 2), *c), S("hi%d" % (t % 2), *c), S("dep", *c)
+        mm([(p, S("px", 128 * k, 128 * k + 128), S("pr", X + k, X2, 16), k == 0, k == 15) for k in range(16)])
+        tt(S("t3", *c), p, um, A.mult)
+        ts(S("q2", *c), p, 32.0, A.mult, float(2464 * t - 131072), A.add)
+        tt(S("t3", *c), S("t3", *c), S("q2", *c), A.add)
+        ts(S("t3", *c), S("t3", *c), 5, A.arith_shift_right, 4095, A.bitwise_and)
+        cp(S("zl", *c), S("t3", *c))
+        tt(S("dif", *c), p, S("vb%d" % t, *c), A.subtract)
+        tt(S("d", X, X2), IND("claimw", 0, 4096, "zl", *c), S("x%d" % (t % 2), X, X2), A.subtract)
+        act(S("ad", X, X2), S("d", X, X2), AF.Abs)
+        mm([(w2, S("sx", 128 * k, 128 * k + 128), S("ad", X + k, X2, 16), k == 0, k == 15) for k in range(16)])
+        ts(dep, w2, S("thc%d" % t, 0, 1), A.is_lt)
+        mm([(w2, full("trim"), dep, True, True), (w3, full("dm32"), dep, True, True)])
+        ts(w2, w2, K16, A.is_equal)
+        tt(S("fh", *c), w2, hi, A.mult)
+        ts(w3, w3, 17.0, A.is_ge)
+        one(w2, full("blkf"), S("fh", *c))
+        tt(S("dlt", *c), w2, hi, A.subtract)
+        tt(w4, w3, S("dlt", *c), A.mult)
+        tt(S("h2f", *c), w4, hi, A.add)
+        cp(S("h2l", *c), S("h2f", *c))
+        act(S("xs", X, X2), IND("claimw", 0, 4096, "h2l", *c), AF.Copy)
+
+    def st_m(t, n):
+        c = BLOCKS[n]
+        X, X2 = 16 * c[0], 16 * c[1]
+        xs = S("xs", X, X2)
+        scan(S("mx", X, X2), S("r1", 0, X2 - X), xs, 0.0, A.mult, A.max)
+        scan(S("mn", X, X2), S("rm", 0, X2 - X), xs, 256.0, A.max, A.min)
+        tt(S("msum", *c), S("mx", X + 15, X2, 16), S("mn", X + 15, X2, 16), A.add)
+        ts(S("mhalf", *c), S("msum", *c), 1, A.arith_shift_right)
+        cp(S("mm_", *c), S("mhalf", *c))
+
+    def st_newnames(t, h):
+        c = (128 * h, 128 * h + 128)
+        tt(S("vm", *c), S("dif", *c), S("dep", *c), A.mult)
+        tt(S("vn%d" % t, *c), S("vm", *c), S("vb%d" % t, *c), A.add)
+        if t < VIS - 1:
+            send("v", t, h)
+            red(S("dsum", h, h + 1), S("dep", *c), A.add)
+
+    def st_count(t):
+        if t == VIS - 1:
+            return
+        mm([(S("pk", 0, 1), full("onesf"), S("dsum", 0, 1), True, False), (S("pk", 0, 1), full("onesf"), S("dsum", 1, 2), False, True)])
+        cp(S("cint", 0, 1), S("pk", 0, 1))
+        ts(S("cint", 1, 2), S("cint", 0, 1), 31, A.bitwise_and)
+        tt(S("thc%d" % (t + 1), 0, 1), S("cint", 1, 2), S("thb", 0, 1), A.add)
+
+    def distances(src, X, mid, out, scale):
+        for q in range(4):
+            b = bank()
+            gr = []
+            for e in range(4):
+                k = 4 * q + e
+                o = S(b, 128 * e, 128 * e + 128)
+                gr += [(o, full("eye"), S(src, X + k, X + 2048, 16), True, False), (o, full("neye"), mid, False, True)]
+            mm(gr)
+            act(S(out, X + 512 * q, X + 512 * q + 512), S(b, 0, 512), AF.Abs, None, scale)
+
+    def st_truth(t, h):
+        c = (128 * h, 128 * h + 128)
+        X = 2048 * h
+        distances("xs", X, S("mm_", *c), "af", 4096.0)
+        K = 128 * h
+        key = S("pk", K, K + 128)
+        mm([(key, full("eye"), full("j1"), True, False), (key, full("eye"), full("j2"), False, False)] +
+           [(key, S("sx", 128 * a, 128 * a + 128), S("af", X + a, X + 2048, 16), False, a == 15) for a in range(16)])
+        B = 256 * h
+        cp(S("tr", B, B + 64), S("pk", K + 64, K + 128))
+        tt(S("tr", B + 64, B + 128), S("pk", K, K + 64), S("tr", B, B + 64), A.min)
+        tt(S("tr", B + 128, B + 160), S("tr", B + 64, B + 96), S("tr", B + 96, B + 128), A.min)
+        tt(S("tr", B + 160, B + 176), S("tr", B + 128, B + 144), S("tr", B + 144, B + 160), A.min)
+        tt(S("kint", 32 * h, 32 * h + 8), S("tr", B + 160, B + 168), S("tr", B + 168, B + 176), A.min)
+        ts(S("kint", 32 * h + 8, 32 * h + 16), S("kint", 32 * h, 32 * h + 8), 4095, A.bitwise_and)
+        cp(S("yl", 8 * h, 8 * h + 8), S("kint", 32 * h + 8, 32 * h + 16))
+        y = S("yy", *c)
+        cp(y, IND("xs", X, X + 2048, "yl", 8 * h, 8 * h + 8))
+        mm([(key, full("eye"), y, True, False), (key, full("eye"), S("yb%d" % t, *c), False, True)])
+        ts(S("yhalf", *c), key, 0.5, A.mult, -0.25, A.add)
+        cp(S("yn%d" % t, *c), S("yhalf", *c))
+        if t < VIS - 1:
+            send("y", t, h)
+
+    def st_err(t, h):
+        c = (128 * h, 128 * h + 128)
+        X = 2048 * h
+        distances("x%d" % (t % 2), X, S("yy", *c), "ae", 32.0)
+        E = 256 + 128 * h
+        ek = S("pk", E, E + 128)
+        mm([(ek, full("eye"), full("kt"), True, False)] +
+           [(S("pk", E + k, E + 128, 16), S("ae", X + 128 * k, X + 128 * k + 128), S("blk", 0, 128, 16), False, k == 15) for k in range(16)])
+        B = 256 * h
+        scan(S("pm", B, B + 128), S("r1", 0, 128), ek, 0.0, A.mult, A.max)
+        tt(S("tt_", 128 * h + 1, 128 * h + 128), S("pk", E + 1, E + 128), S("pm", B, B + 127), A.min)
+        scan(S("pm", B + 129, B + 256), S("r2", 1, 128), S("tt_", 128 * h + 1, 128 * h + 128), 0.0, A.mult, A.max)
+        m = S("pm", B + 15, B + 256, 16)
+        cp(S("code", 32 * h, 32 * h + 16), m)
+        tt(S("ask", 16 * h, 16 * h + 16), m, full("tht"), A.is_ge)
+        ts(S("code", 32 * h + 16, 32 * h + 32), S("code", 32 * h, 32 * h + 16), 31, A.bitwise_and)
+        tt(S("kk", 16 * h, 16 * h + 16), S("code", 32 * h + 16, 32 * h + 32), S("ask", 16 * h, 16 * h + 16), A.mult)
+        one(S("pa", 0, 128, 1, 16), S("kk", 16 * h, 16 * h + 16), full("eye"))
+        kt = S("ktb", 128 * h, 128 * h + 128, 1, 16)
+        act(kt, S("pa", 0, 128, 1, 16), AF.Copy)
+        RA, RB, C, N = S("pa", 128, 256), S("pa", 256, 384), S("pa", 384, 512), S("pa", 0, 128)
+        mm([(RB, S("exs", 384, 512, 1, 16), kt, True, True), (RA, S("exs", 128, 256, 1, 16), kt, True, True)])
+        v = S("vb%d" % t, *c)
+        ts(S("ohb", *c), RB, CODE, A.is_equal)
+        tt(S("sb", *c), S("ohb", *c), v, A.mult)
+        mm([(C, full("blk512"), S("sb", *c), True, False), (C, full("blk8k"), S("ohb", *c), False, False), (C, full("eye"), S("oc", *c), False, True)])
+        act(S("cr", *c), C, AF.Copy)
+        tt(S("dg", *c), C, full("dmask"), A.mult)
+        scan(S("cs", *c), S("r1", 0, 128), S("dg", *c), 0.0, A.mult, A.add)
+        lst = S("cs", 128 * h + 15, 128 * h + 128, 16)
+        ts(S("bia", 8 * h, 8 * h + 8), lst, -1.0, A.mult, 128.0, A.add)
+        for b in range(8 * h, 8 * h + 8):
+            w = 16 * b + 16
+            act(S("dd", 256 * b, 256 * b + w), S("cr", 0, w), AF.Identity, S("bia", b, b + 1), 1.0)
+            red(S("dmin", b, b + 1), S("dd", 256 * b, 256 * b + w), A.min, True)
+        ts(RA, RA, CODE, A.is_equal)
+        tt(S("sa", *c), RA, v, A.mult)
+        one(N, full("blkf"), S("sa", *c))
+        ts(S("aint", *c), N, ACS, A.mult, ACB, A.add)
+        ts(S("aint", *c), S("aint", *c), 255, A.bitwise_and)
+        cp(S("adat", *c), S("aint", *c))
+        cp(S("sint", 16 * h, 16 * h + 8), lst)
+        ts(S("sint", 16 * h + 8, 16 * h + 16), S("sint", 16 * h, 16 * h + 8), 9, A.logical_shift_right)
+        ts(S("dfl", 32 * h, 32 * h + 8), S("dmin", 8 * h, 8 * h + 8), 128.0, A.is_lt)
+        tt(S("dfl", 32 * h + 8, 32 * h + 16), S("dfl", 32 * h, 32 * h + 8), S("dcon", 8 * h, 8 * h + 8), A.mult)
+        tt(S("dfl", 32 * h + 16, 32 * h + 24), S("sint", 16 * h + 8, 16 * h + 16), S("dfl", 32 * h + 8, 32 * h + 16), A.max)
+        cp(S("ol", 8 * h, 8 * h + 8), S("dfl", 32 * h + 16, 32 * h + 24))
+
+    def st_scatter(t, h):
+        c = (128 * h, 128 * h + 128)
+        cp(IND("parw", 0, 4368, "ol", 8 * h, 8 * h + 8), S("adat", *c))
+
+    nb = len(BLOCKS)
+    for t in range(VIS):
+        for h in range(2):
+            st_names(t, h)
+        for h in range(2):
+            st_hash(t, h)
+            st_xgather(t, h)
+        for n in range(nb):
+            st_pgather(t, n)
+        for h in range(2):
+            for n in range(h * nb // 2, (h + 1) * nb // 2):
+                st_z(t, n)
+                st_m(t, n)
+            st_newnames(t, h)
+        st_count(t)
+        for h in range(2):
+            st_truth(t, h)
+        for h in range(2):
+            st_err(t, h)
+        for h in range(2):
+            st_scatter(t, h)
+    for h in range(2):
+        c = (128 * h, 128 * h + 128)
+        dma("Y", "l_yv%d" % h, [(lambda T, c=c: T.yv[:, c[0]:c[1]], lambda T, c=c: T.vn4[:, c[0]:c[1]])], [S("vn4", *c)], [], 2.0)
+        dma("Y", "l_ye%d" % h, [(lambda T, c=c: T.ye[:, c[0]:c[1]], lambda T, c=c: T.yn4[:, c[0]:c[1]])], [S("yn4", *c)], [], 2.0)
+    mm([(S("pu", 0, 256), S("px", 128 * k, 128 * k + 128), S("parw", 16 + 256 * k, 272 + 256 * k), k == 0, k == 15) for k in range(16)])
+    cp(full("ypf"), S("pu", 0, 256))
+    dma("Y", "l_yp", [(lambda T: T.yp[:], lambda T: T.ypf[:])], [full("ypf")], [], 2.0)
+
+    hist = {}
+    for i, o in enumerate(ops):
+        dep = set()
+        for (n, a, b) in o["R"]:
+            ps = BUF[n][0] == "psum"
+            for (j, a2, b2, w) in hist.get(n, ()):
+                if (w and a < b2 and a2 < b) or (ps and ops[j]["q"] != o["q"]):
+                    dep.add(j)
+        for (n, a, b) in o["W"]:
+            ps = BUF[n][0] == "psum"
+            for (j, a2, b2, w) in hist.get(n, ()):
+                if (a < b2 and a2 < b) or (ps and ops[j]["q"] != o["q"]):
+                    dep.add(j)
+        for (n, a, b) in o["R"]:
+            hist.setdefault(n, []).append((i, a, b, False))
+        for (n, a, b) in o["W"]:
+            l = hist.setdefault(n, [])
+            l[:] = [e for e in l if not (a <= e[1] and e[2] <= b) or BUF[n][0] == "psum"]
+            l.append((i, a, b, True))
+        if o["q"] == "N":
+            dep = {o["send"]}
+        dep.discard(i)
+        o["D"] = dep
+    return ops
+
+
+def schedule(ops, seed=0, eps=0.0):
+    n = len(ops)
+    succ = [[] for _ in range(n)]
+    for i, o in enumerate(ops):
+        for j in o["D"]:
+            succ[j].append(i)
+    prio = [0.0] * n
+    rnd = np.random.default_rng(seed).random(n)
+    for i in range(n - 1, -1, -1):
+        prio[i] = ops[i]["c"] + max([prio[j] + LAT for j in succ[i]], default=0.0)
+    key = [(-(prio[i] + eps * float(rnd[i])), i) for i in range(n)]
+    left = [len(o["D"]) for o in ops]
+    heap = sorted(key[i] for i in range(n) if left[i] == 0)
+    busy = {}
+    est, fin = [0.0] * n, [0.0] * n
+    order = []
+    while heap:
+        i = heap.pop(0)[1]
+        o = ops[i]
+        t = est[i]
+        if o["q"] != "N":
+            occ = 0.15 if o["sem"] and o["q"] in "YS" else o["c"]
+            b = busy.setdefault(o["q"], [])
+            at = len(b)
+            while at > 0 and b[at - 1][1] > t:
+                at -= 1
+            while at < len(b) and max(t, b[at - 1][1] if at else 0.0) + occ > b[at][0]:
+                at += 1
+            t = max(t, b[at - 1][1] if at else 0.0)
+            b.insert(at, (t, t + occ))
+        o["start"] = t
+        fin[i] = t + o["c"]
+        order.append((t, len(order), i))
+        for j in succ[i]:
+            est[j] = max(est[j], fin[i] + LAT)
+            left[j] -= 1
+            if left[j] == 0:
+                lo, hi = 0, len(heap)
+                while lo < hi:
+                    mid = (lo + hi) // 2
+                    if heap[mid] < key[j]:
+                        lo = mid + 1
+                    else:
+                        hi = mid
+                heap.insert(lo, key[j])
+    order.sort()
+    return [i for _, _, i in order], max(fin)
+
+
+SEMQ = {"V": "vv", "S": "ss", "P": "pp", "G": "gg"}
+
+
+def plan(nE):
+    if nE in _CACHE:
+        return _CACHE[nE]
+    ops = build(nE)
+    order, total = schedule(ops, SEED, EPS)
+    count = {s: 0 for s in SEMQ.values()}
+    know, kq, out = {}, {}, []
+    for i in order:
+        o = ops[i]
+        q = o["q"]
+        mine = kq.setdefault(q, {})
+        waits = {}
+        if q != "N":
+            for j in sorted(o["D"], key=lambda j: -ops[j]["start"]):
+                s, v = ops[j]["ev"]
+                if mine.get(s, 0) >= v:
+                    continue
+                waits[s] = max(waits.get(s, 0), v)
+                for s2, v2 in know[j].items():
+                    mine[s2] = max(mine.get(s2, 0), v2)
+                mine[s] = max(mine.get(s, 0), v)
+        know[i] = dict(mine) if q != "N" else {}
+        if o["sem"]:
+            o["ev"] = (o["sem"], o["val"])
+        else:
+            s = SEMQ[q]
+            count[s] += len(o["f"])
+            o["ev"] = (s, count[s])
+        out.append((o, sorted(waits.items())))
+    ends = {}
+    for o in ops:
+        s, v = o["ev"]
+        ends[s] = max(ends.get(s, 0), v)
+    _CACHE[nE] = (out, ends, total)
+    return _CACHE[nE]
+
+
+def rank_program(g, core, T, topo):
+    rank = T.rank_of(core)
+    if rank is None:
+        return
+    nxt = T.cores[(rank + 1) % len(T.cores)]
+    eng = topo.engines(core, nxt)[::2]
+    mask = 0
+    for e in eng:
+        mask |= 1 << e
+    rid, pid, _ = topo.addr(nxt)
+    steps, ends, _ = plan(len(eng))
+    queue = {"V": g.vector, "S": g.scalar, "P": g.tensor, "G": g, "Y": g.sync}
+    for o, waits in steps:
+        q = o["q"]
+        if q == "N":
+            continue
+        for s, v in waits:
+            queue[q].wait_ge(T.sem[s], v)
+        if o["send"]:
+            k, t, h = o["send"]
+            c = slice(128 * h, 128 * h + 128)
+            g.remote_dma(out_ap=T["%sb%d" % (k, t)][:, c], in_ap=T["%sn%d" % (k, t - 1)][:, c], remote_sem=T.sem["a%s%d%d" % (k, t, h)],
+                         local_sem=T.sem["o%s%d%d" % (k, t, h)], pid=pid, routing_id=rid, dma_engine_mask=mask)
+        elif o["sem"]:
+            for f in o["f"]:
+                f(g, T).then_inc(T.sem[o["sem"]], 16)
+        else:
+            for f in o["f"]:
+                f(g, T).then_inc(T.sem[SEMQ[q]], 1)
+    for s, v in sorted(ends.items()):
+        g.wait_ge(T.sem[s], v)

@@ -42,8 +42,14 @@ _b("kk", [128, 32], BF)
 _b("ktb", [16, 256], BF)
 _b("bia", [128, 16], F32)
 _b("sint", [128, 32], I32)
-_b("dd", [128, 4096], F32)
-_b("dmin", [128, 16], F32)
+_b("dd", [128, 3072], BF)
+_b("dso", [128, 3072], BF)
+_b("rs0", [128, 512], BF)
+_b("rs1", [128, 1024], BF)
+_b("px32", [128, 2048], BF)
+_b("cb", [128, 64], BF)
+for _t in range(VIS):
+    _b("ct%d" % _t, [128, 64], BF)
 _b("dfl", [128, 64], F32)
 _b("ol", [128, 16], U16)
 _b("dsum", [128, 2], F32)
@@ -77,7 +83,7 @@ _b("parb", [128, 512], BF)
 _b("ypf", [128, 256], F32)
 _b("dlo", [8, 4096], BF, "dram")
 _b("dhi", [8, 4096], BF, "dram")
-for _n in ("pz0", "pz1", "pu", "pk", "pa", "pf0", "pf1", "pf2"):
+for _n in ("pz0", "pz1", "pz2", "pz3", "pk0", "pk1", "pf0", "pf1"):
     _b(_n, [128, 512], F32, "psum")
 
 for _n in ("who", "est", "wt", "lim", "par", "claim0", "claim1", "plo", "phi", "pwin", "yv0", "yv1", "ye0", "ye1", "yp"):
@@ -101,9 +107,13 @@ for _d in _ROOM:
     SCRATCH["pack_" + _d] = ("sbuf", [128, _ROOM[_d]], _d)
 
 _CACHE = {}
-CY, PCY, GATH, SCAT = 0.001, 0.0006, 1.55, 3.5
-VOV, SOV, POV, LAT = 0.03, 0.04, 0.03, 0.1
+CY, PCY, GATH, SCAT = 0.00083 * 1.1, 0.00042 * 1.1, 1.5, 3.5
+VOV, SOV, POV, LAT = 0.04, 0.04, 0.02, 0.12
 SEED, EPS = 0, 0.0
+ONV = ()
+LEAD = {"x0": 2.7, "t1": 1.3, "t0": -0.4, "x1": 0.0, "n1": 1.3, "z0": -0.2, "m1": -0.6, "p0": 2.9, "w1": -1.1, "p1": -0.1, "w0": -3.1, "e1": -0.6, "n0": 0.6, "m0": 1.2, "z1": 0.4, "e0": -0.3}
+BONUS = {}
+ERRB = (("pf0", "pf1"), ("pf0", "pf1"))
 XL = 64
 
 
@@ -145,12 +155,14 @@ def half(*ss):
 
 def build(nE):
     ops = []
+    since = [100000]
+    part = [""]
 
     def add(q, fns, R, W, cost, sem=None, val=0, send=None):
         rr = [r for s in R for r in regs(s)]
         ww = [(s[0], s[1], s[2]) for s in W]
         offs = [(s[3], s[4], s[5]) for s in W if len(s) == 7]
-        ops.append({"q": q, "f": fns, "R": rr + offs, "W": ww, "c": cost, "sem": sem, "val": val, "send": send})
+        ops.append({"q": q, "f": fns, "R": rr + offs, "W": ww, "c": cost, "sem": sem, "val": val, "send": send, "at": len(ops) - since[0], "part": part[0]})
         return len(ops) - 1
 
     def vcost(n, f=1.0):
@@ -204,6 +216,12 @@ def build(nE):
                 kw["scale"] = scale
             return g.scalar.activation(out=ap(T, out), in_=ap(T, a), func=func, **kw)
         add("S", [f], R, [out], max(64, width(a) * (GATH if len(a) == 7 else 1.0)) * CY + SOV)
+
+    def gather(tag, out, a):
+        if tag in ONV:
+            cp(out, a)
+        else:
+            act(out, a, AF.Copy)
 
     def mm(groups):
         fns = []
@@ -289,20 +307,21 @@ def build(nE):
     cp(full("onesf"), full("ones"))
     cp(full("eyef"), S("eye", 0, 16, 1, 16))
     ts(full("limd"), S("eyef", 0, 8, 1, 8), S("limf", 1, 2, 1, 8), A.mult, 32.0, A.mult)
-    mm([(S("pa", 0, 2), S("exf", 0, 128, 1, 8), full("limf"), True, True),
-        (S("pa", 8, 16), S("onesf", 0, 128, 1, 8), full("limd"), True, True)])
-    cp(full("thb"), S("pa", 0, 2))
-    cp(S("thc0", 0, 1), S("pa", 0, 1))
+    mm([(S("pk1", 0, 2), S("exf", 0, 128, 1, 8), full("limf"), True, True),
+        (S("pk1", 8, 16), S("onesf", 0, 128, 1, 8), full("limd"), True, True)])
+    cp(full("thb"), S("pk1", 0, 2))
+    cp(S("thc0", 0, 1), S("pk1", 0, 1))
     fill(S("tht", 0, 8), -1.0)
-    cp(S("tht", 8, 16), S("pa", 8, 16))
+    cp(S("tht", 8, 16), S("pk1", 8, 16))
     cp(full("blkf"), full("blk"))
     fill(full("r1"), 1.0)
     ts(S("r1", 0, 2048, 16), S("r1", 0, 2048, 16), 0.0, A.mult)
     fill(full("rm"), 0.0)
     ts(S("rm", 0, 2048, 16), S("rm", 0, 2048, 16), 256.0, A.add)
-    iota(full("io1"), [[0, 16], [256, 8]], 0, 0)
-    ts(full("j1"), full("io1"), COLA, A.add)
-    iota(full("j2"), [[1, 16], [0, 8]], 0, 0)
+    QB = (BLOCKS[0][1] - BLOCKS[0][0]) // 16
+    iota(S("io1", 0, 16 * QB), [[0, 16], [256, QB]], 0, 0)
+    ts(S("j1", 0, 16 * QB), S("io1", 0, 16 * QB), COLA, A.add)
+    iota(S("j2", 0, 16 * QB), [[1, 16], [0, QB]], 0, 0)
     iota(full("kt"), [[0, 8], [-1, 16]], 16, 0)
     iota(full("oc"), [[1, 256]], 0, 0)
     fill(full("r2"), 1.0)
@@ -314,11 +333,20 @@ def build(nE):
     ts(full("blk8k"), full("blk"), 8192.0, A.mult)
     iota(full("iod"), [[16, 16]], 4112, 0)
     ts(full("dcon"), full("iod"), K16, A.add)
+    ts(full("px32"), full("px"), 32.0, A.mult)
+    fill(full("cb"), -131072.0)
+    for t in range(VIS):
+        fill(full("ct%d" % t), float(2464 * t))
+    fill(full("dd"), 4194304.0)
+    for h in range(2):
+        n, w = 512 + 512 * h, 128 + 128 * h
+        fill(full("rs%d" % h), 0.0)
+        ts(S("rs%d" % h, 0, n, w), S("rs%d" % h, 0, n, w), 4194304.0, A.add)
     turn = [0]
 
-    def bank():
+    def bank(names):
         turn[0] += 1
-        return "pf%d" % (turn[0] % 3)
+        return names[turn[0] % 2]
 
     def send(what, t, h):
         c = (128 * h, 128 * h + 128)
@@ -336,7 +364,7 @@ def build(nE):
     def st_hash(t, h):
         c = (128 * h, 128 * h + 128)
         um, hi = S("um%d" % (t % 2), *c), S("hi%d" % (t % 2), *c)
-        U, W = S("pu", 256 * h, 256 * h + 128), S("pu", 256 * h + 128, 256 * h + 256)
+        U, W = S("pz%d" % (2 * h), 256, 384), S("pz%d" % (2 * h), 384, 512)
         one(U, full("wmat"), S("yb%d" % t, *c))
         cp(S("t1", *c), U)
         ts(um, S("t1", *c), 4095, A.bitwise_and)
@@ -348,23 +376,25 @@ def build(nE):
     def st_xgather(t, h):
         c = (128 * h, 128 * h + 128)
         for a in range(c[0], c[1], XL):
-            act(S("x%d" % (t % 2), 16 * a, 16 * (a + XL)), IND("claimw", 0, 4096, "hl", a, a + XL), AF.Copy)
+            gather("x%d" % (a // XL), S("x%d" % (t % 2), 16 * a, 16 * (a + XL)), IND("claimw", 0, 4096, "hl", a, a + XL))
 
     def st_pgather(t, n):
         c = BLOCKS[n]
-        act(S("pr", 16 * c[0], 16 * c[1]), IND("parw", 16, 4112, "vl", *c), AF.Copy)
+        gather("p%d" % n, S("pr", 16 * c[0], 16 * c[1]), IND("parw", 16, 4112, "vl", *c))
 
     def st_z(t, n):
         c = BLOCKS[n]
         L = c[1] - c[0]
         X, X2 = 16 * c[0], 16 * c[1]
-        b = "pz%d" % (n % 2)
-        p, w2, w3, w4 = [S(b, 128 * e, 128 * e + L) for e in range(4)]
+        b = "pz%d" % n
+        p, w2, w3, q = [S(b, 64 * e, 64 * e + L) for e in range(4)]
+        w4 = q
         um, hi, dep = S("um%d" % (t % 2), *c), S("hi%d" % (t % 2), *c), S("dep", *c)
         mm([(p, S("px", 128 * k, 128 * k + 128), S("pr", X + k, X2, 16), k == 0, k == 15) for k in range(16)])
-        tt(S("t3", *c), p, um, A.mult)
-        ts(S("q2", *c), p, 32.0, A.mult, float(2464 * t - 131072), A.add)
-        tt(S("t3", *c), S("t3", *c), S("q2", *c), A.add)
+        mm([(q, full("eye"), full("cb"), True, False), (q, full("eye"), full("ct%d" % t), False, False)] +
+           [(q, S("px32", 128 * k, 128 * k + 128), S("pr", X + k, X2, 16), False, k == 15) for k in range(16)])
+        tt(S("q2", *c), p, um, A.mult)
+        tt(S("t3", *c), q, S("q2", *c), A.add)
         ts(S("t3", *c), S("t3", *c), 5, A.arith_shift_right, 4095, A.bitwise_and)
         cp(S("zl", *c), S("t3", *c))
         tt(S("dif", *c), p, S("vb%d" % t, *c), A.subtract)
@@ -381,7 +411,7 @@ def build(nE):
         tt(w4, w3, S("dlt", *c), A.mult)
         tt(S("h2f", *c), w4, hi, A.add)
         cp(S("h2l", *c), S("h2f", *c))
-        act(S("xs", X, X2), IND("claimw", 0, 4096, "h2l", *c), AF.Copy)
+        gather("s%d" % n, S("xs", X, X2), IND("claimw", 0, 4096, "h2l", *c))
 
     def st_m(t, n):
         c = BLOCKS[n]
@@ -389,8 +419,9 @@ def build(nE):
         xs = S("xs", X, X2)
         scan(S("mx", X, X2), S("r1", 0, X2 - X), xs, 0.0, A.mult, A.max)
         scan(S("mn", X, X2), S("rm", 0, X2 - X), xs, 256.0, A.max, A.min)
-        tt(S("msum", *c), S("mx", X + 15, X2, 16), S("mn", X + 15, X2, 16), A.add)
-        ts(S("mhalf", *c), S("msum", *c), 1, A.arith_shift_right)
+        w = S("pz%d" % n, 64, 64 + c[1] - c[0])
+        mm([(w, full("eye"), S("mx", X + 15, X2, 16), True, False), (w, full("eye"), S("mn", X + 15, X2, 16), False, True)])
+        ts(S("mhalf", *c), w, 0.5, A.mult, -0.25, A.add)
         cp(S("mm_", *c), S("mhalf", *c))
 
     def st_newnames(t, h):
@@ -404,41 +435,50 @@ def build(nE):
     def st_count(t):
         if t == VIS - 1:
             return
-        mm([(S("pk", 0, 1), full("onesf"), S("dsum", 0, 1), True, False), (S("pk", 0, 1), full("onesf"), S("dsum", 1, 2), False, True)])
-        cp(S("cint", 0, 1), S("pk", 0, 1))
+        mm([(S("pk0", 0, 1), full("onesf"), S("dsum", 0, 1), True, False), (S("pk0", 0, 1), full("onesf"), S("dsum", 1, 2), False, True)])
+        cp(S("cint", 0, 1), S("pk0", 0, 1))
         ts(S("cint", 1, 2), S("cint", 0, 1), 31, A.bitwise_and)
         tt(S("thc%d" % (t + 1), 0, 1), S("cint", 1, 2), S("thb", 0, 1), A.add)
 
-    def distances(src, X, mid, out, scale):
-        for q in range(4):
-            b = bank()
+    def distances(src, X, mid, out, scale, banks):
+        L = width(mid)
+        K = 512 // L
+        for q in range(16 // K):
+            b = bank(banks)
             gr = []
-            for e in range(4):
-                k = 4 * q + e
-                o = S(b, 128 * e, 128 * e + 128)
-                gr += [(o, full("eye"), S(src, X + k, X + 2048, 16), True, False), (o, full("neye"), mid, False, True)]
+            for e in range(K):
+                k = K * q + e
+                o = S(b, L * e, L * e + L)
+                gr += [(o, full("eye"), S(src, X + k, X + 16 * L, 16), True, False), (o, full("neye"), mid, False, True)]
             mm(gr)
             act(S(out, X + 512 * q, X + 512 * q + 512), S(b, 0, 512), AF.Abs, None, scale)
 
-    def st_truth(t, h):
+    def st_truth(t, n):
+        c = BLOCKS[n]
+        L = c[1] - c[0]
+        X, X2, Q, h = 16 * c[0], 16 * c[1], L // 16, c[0] // 128
+        distances("xs", X, S("mm_", *c), "af", 4096.0, ("pf0", "pf1"))
+        bk, K = "pk%d" % h, c[0] % 128
+        key = S(bk, K, K + L)
+        mm([(key, full("eye"), S("j1", 0, L), True, False), (key, full("eye"), S("j2", 0, L), False, False)] +
+           [(key, S("sx", 128 * a, 128 * a + 128), S("af", X + a, X2, 16), False, a == 15) for a in range(16)])
+        B = 2 * c[0]
+        cp(S("tr", B, B + L // 2), S(bk, K + L // 2, K + L))
+        tt(S("tr", B + L // 2, B + L), S(bk, K, K + L // 2), S("tr", B, B + L // 2), A.min)
+        a, w = B + L // 2, L // 4
+        while w > Q:
+            tt(S("tr", a + 2 * w, a + 3 * w), S("tr", a, a + w), S("tr", a + w, a + 2 * w), A.min)
+            a, w = a + 2 * w, w // 2
+        I = c[0] // 4
+        tt(S("kint", I, I + Q), S("tr", a, a + w), S("tr", a + w, a + 2 * w), A.min)
+        ts(S("kint", I + Q, I + 2 * Q), S("kint", I, I + Q), 4095, A.bitwise_and)
+        cp(S("yl", c[0] // 16, c[1] // 16), S("kint", I + Q, I + 2 * Q))
+        cp(S("yy", *c), IND("xs", X, X2, "yl", c[0] // 16, c[1] // 16))
+
+    def st_est(t, h):
         c = (128 * h, 128 * h + 128)
-        X = 2048 * h
-        distances("xs", X, S("mm_", *c), "af", 4096.0)
-        K = 128 * h
-        key = S("pk", K, K + 128)
-        mm([(key, full("eye"), full("j1"), True, False), (key, full("eye"), full("j2"), False, False)] +
-           [(key, S("sx", 128 * a, 128 * a + 128), S("af", X + a, X + 2048, 16), False, a == 15) for a in range(16)])
-        B = 256 * h
-        cp(S("tr", B, B + 64), S("pk", K + 64, K + 128))
-        tt(S("tr", B + 64, B + 128), S("pk", K, K + 64), S("tr", B, B + 64), A.min)
-        tt(S("tr", B + 128, B + 160), S("tr", B + 64, B + 96), S("tr", B + 96, B + 128), A.min)
-        tt(S("tr", B + 160, B + 176), S("tr", B + 128, B + 144), S("tr", B + 144, B + 160), A.min)
-        tt(S("kint", 32 * h, 32 * h + 8), S("tr", B + 160, B + 168), S("tr", B + 168, B + 176), A.min)
-        ts(S("kint", 32 * h + 8, 32 * h + 16), S("kint", 32 * h, 32 * h + 8), 4095, A.bitwise_and)
-        cp(S("yl", 8 * h, 8 * h + 8), S("kint", 32 * h + 8, 32 * h + 16))
-        y = S("yy", *c)
-        cp(y, IND("xs", X, X + 2048, "yl", 8 * h, 8 * h + 8))
-        mm([(key, full("eye"), y, True, False), (key, full("eye"), S("yb%d" % t, *c), False, True)])
+        key = S("pk%d" % h, 384, 512)
+        mm([(key, full("eye"), S("yy", *c), True, False), (key, full("eye"), S("yb%d" % t, *c), False, True)])
         ts(S("yhalf", *c), key, 0.5, A.mult, -0.25, A.add)
         cp(S("yn%d" % t, *c), S("yhalf", *c))
         if t < VIS - 1:
@@ -447,24 +487,24 @@ def build(nE):
     def st_err(t, h):
         c = (128 * h, 128 * h + 128)
         X = 2048 * h
-        distances("x%d" % (t % 2), X, S("yy", *c), "ae", 32.0)
-        E = 256 + 128 * h
-        ek = S("pk", E, E + 128)
+        distances("x%d" % (t % 2), X, S("yy", *c), "ae", 32.0, ERRB[h])
+        bk, ba, E = "pk%d" % h, "pz%d" % (2 * h + 1), 256
+        ek = S(bk, E, E + 128)
         mm([(ek, full("eye"), full("kt"), True, False)] +
-           [(S("pk", E + k, E + 128, 16), S("ae", X + 128 * k, X + 128 * k + 128), S("blk", 0, 128, 16), False, k == 15) for k in range(16)])
+           [(S(bk, E + k, E + 128, 16), S("ae", X + 128 * k, X + 128 * k + 128), S("blk", 0, 128, 16), False, k == 15) for k in range(16)])
         B = 256 * h
         scan(S("pm", B, B + 128), S("r1", 0, 128), ek, 0.0, A.mult, A.max)
-        tt(S("tt_", 128 * h + 1, 128 * h + 128), S("pk", E + 1, E + 128), S("pm", B, B + 127), A.min)
+        tt(S("tt_", 128 * h + 1, 128 * h + 128), S(bk, E + 1, E + 128), S("pm", B, B + 127), A.min)
         scan(S("pm", B + 129, B + 256), S("r2", 1, 128), S("tt_", 128 * h + 1, 128 * h + 128), 0.0, A.mult, A.max)
         m = S("pm", B + 15, B + 256, 16)
         cp(S("code", 32 * h, 32 * h + 16), m)
         tt(S("ask", 16 * h, 16 * h + 16), m, full("tht"), A.is_ge)
         ts(S("code", 32 * h + 16, 32 * h + 32), S("code", 32 * h, 32 * h + 16), 31, A.bitwise_and)
         tt(S("kk", 16 * h, 16 * h + 16), S("code", 32 * h + 16, 32 * h + 32), S("ask", 16 * h, 16 * h + 16), A.mult)
-        one(S("pa", 0, 128, 1, 16), S("kk", 16 * h, 16 * h + 16), full("eye"))
+        one(S(ba, 0, 128, 1, 16), S("kk", 16 * h, 16 * h + 16), full("eye"))
         kt = S("ktb", 128 * h, 128 * h + 128, 1, 16)
-        act(kt, S("pa", 0, 128, 1, 16), AF.Copy)
-        RA, RB, C, N = S("pa", 128, 256), S("pa", 256, 384), S("pa", 384, 512), S("pa", 0, 128)
+        act(kt, S(ba, 0, 128, 1, 16), AF.Copy)
+        RA, RB, C, N = S(ba, 128, 256), S(ba, 256, 384), S(ba, 384, 512), S(ba, 0, 128)
         mm([(RB, S("exs", 384, 512, 1, 16), kt, True, True), (RA, S("exs", 128, 256, 1, 16), kt, True, True)])
         v = S("vb%d" % t, *c)
         ts(S("ohb", *c), RB, CODE, A.is_equal)
@@ -475,10 +515,14 @@ def build(nE):
         scan(S("cs", *c), S("r1", 0, 128), S("dg", *c), 0.0, A.mult, A.add)
         lst = S("cs", 128 * h + 15, 128 * h + 128, 16)
         ts(S("bia", 8 * h, 8 * h + 8), lst, -1.0, A.mult, 128.0, A.add)
+        D0, DW = 1024 * h, 128 + 128 * h
         for b in range(8 * h, 8 * h + 8):
             w = 16 * b + 16
-            act(S("dd", 256 * b, 256 * b + w), S("cr", 0, w), AF.Identity, S("bia", b, b + 1), 1.0)
-            red(S("dmin", b, b + 1), S("dd", 256 * b, 256 * b + w), A.min, True)
+            at = D0 + DW * (b - 8 * h)
+            act(S("dd", at, at + w), S("cr", 0, w), AF.Abs, S("bia", b, b + 1), 1.0)
+            if b % 4 == 3:
+                at += DW - 4 * DW
+                scan(S("dso", at, at + 4 * DW), full("rs%d" % h), S("dd", at, at + 4 * DW), 0.0, A.max, A.min)
         ts(RA, RA, CODE, A.is_equal)
         tt(S("sa", *c), RA, v, A.mult)
         one(N, full("blkf"), S("sa", *c))
@@ -487,7 +531,7 @@ def build(nE):
         cp(S("adat", *c), S("aint", *c))
         cp(S("sint", 16 * h, 16 * h + 8), lst)
         ts(S("sint", 16 * h + 8, 16 * h + 16), S("sint", 16 * h, 16 * h + 8), 9, A.logical_shift_right)
-        ts(S("dfl", 32 * h, 32 * h + 8), S("dmin", 8 * h, 8 * h + 8), 128.0, A.is_lt)
+        ts(S("dfl", 32 * h, 32 * h + 8), S("dso", D0 + DW - 1, D0 + 8 * DW, DW), 128.0, A.is_lt)
         tt(S("dfl", 32 * h + 8, 32 * h + 16), S("dfl", 32 * h, 32 * h + 8), S("dcon", 8 * h, 8 * h + 8), A.mult)
         tt(S("dfl", 32 * h + 16, 32 * h + 24), S("sint", 16 * h + 8, 16 * h + 16), S("dfl", 32 * h + 8, 32 * h + 16), A.max)
         cp(S("ol", 8 * h, 8 * h + 8), S("dfl", 32 * h + 16, 32 * h + 24))
@@ -498,31 +542,43 @@ def build(nE):
 
     nb = len(BLOCKS)
     for t in range(VIS):
+        since[0] = len(ops)
         for h in range(2):
+            part[0] = "x%d" % h
             st_names(t, h)
         for h in range(2):
+            part[0] = "x%d" % h
             st_hash(t, h)
             st_xgather(t, h)
         for n in range(nb):
+            part[0] = "p%d" % (2 * n // nb)
             st_pgather(t, n)
         for h in range(2):
             for n in range(h * nb // 2, (h + 1) * nb // 2):
+                part[0] = "z%d" % h
                 st_z(t, n)
+                part[0] = "m%d" % h
                 st_m(t, n)
+            part[0] = "n%d" % h
             st_newnames(t, h)
         st_count(t)
         for h in range(2):
-            st_truth(t, h)
+            part[0] = "t%d" % h
+            for n in range(h * nb // 2, (h + 1) * nb // 2):
+                st_truth(t, n)
+            st_est(t, h)
         for h in range(2):
+            part[0] = "e%d" % h
             st_err(t, h)
         for h in range(2):
+            part[0] = "w%d" % h
             st_scatter(t, h)
     for h in range(2):
         c = (128 * h, 128 * h + 128)
         dma("Y", "l_yv%d" % h, [(lambda T, c=c: T.yv[:, c[0]:c[1]], lambda T, c=c: T.vn4[:, c[0]:c[1]])], [S("vn4", *c)], [], 2.0)
         dma("Y", "l_ye%d" % h, [(lambda T, c=c: T.ye[:, c[0]:c[1]], lambda T, c=c: T.yn4[:, c[0]:c[1]])], [S("yn4", *c)], [], 2.0)
-    mm([(S("pu", 0, 256), S("px", 128 * k, 128 * k + 128), S("parw", 16 + 256 * k, 272 + 256 * k), k == 0, k == 15) for k in range(16)])
-    cp(full("ypf"), S("pu", 0, 256))
+    mm([(S("pf0", 0, 256), S("px", 128 * k, 128 * k + 128), S("parw", 16 + 256 * k, 272 + 256 * k), k == 0, k == 15) for k in range(16)])
+    cp(full("ypf"), S("pf0", 0, 256))
     dma("Y", "l_yp", [(lambda T: T.yp[:], lambda T: T.ypf[:])], [full("ypf")], [], 2.0)
 
     hist = {}
@@ -561,7 +617,7 @@ def schedule(ops, seed=0, eps=0.0):
     rnd = np.random.default_rng(seed).random(n)
     for i in range(n - 1, -1, -1):
         prio[i] = ops[i]["c"] + max([prio[j] + LAT for j in succ[i]], default=0.0)
-    key = [(-(prio[i] + eps * float(rnd[i])), i) for i in range(n)]
+    key = [(-(prio[i] + BONUS.get(ops[i]["at"], 0.0) + LEAD.get(ops[i]["part"], 0.0) + eps * float(rnd[i])), i) for i in range(n)]
     left = [len(o["D"]) for o in ops]
     heap = sorted(key[i] for i in range(n) if left[i] == 0)
     busy = {}

import numpy as np
from concourse.mybir import AluOpType, AxisListType, ActivationFunctionType

A = AluOpType
AF = ActivationFunctionType
VIS = 5
BLOCKS = [(0, 64), (64, 128), (128, 192), (192, 256)]
BUF = {}
SEMAPHORES = ["vv", "ss", "pp", "gg"]


def _b(name, shape, dtype="float32", where="sbuf"):
    BUF[name] = (where, shape, dtype)


BF, F32, I32, U16 = "bfloat16", "float32", "int32", "uint16"
_b("claimw", [128, 4096], BF)
_b("parw", [128, 4368], BF)
for _t in range(VIS):
    _b("yb%d" % _t, [128, 256], BF)
    _b("vb%d" % _t, [128, 256], F32)
    _b("yn%d" % _t, [128, 256], BF)
    _b("vn%d" % _t, [128, 256], F32)
    _b("thc%d" % _t, [128, 8], F32)
for _n in ("x0", "x1", "xs", "pr", "d", "ad", "af", "ae", "mx", "mn"):
    _b(_n, [128, 4096], BF)
for _n in ("um0", "um1", "hi0", "hi1", "t1", "t2", "t3", "msum", "mhalf", "yhalf", "aint"):
    _b(_n, [128, 256], I32)
for _n in ("hl", "zl", "vl", "h2l"):
    _b(_n, [128, 256], U16)
for _n in ("q1", "q2", "dif", "vm", "fh", "dlt", "h2f", "sa", "sb", "cr", "dg", "cs", "tt_"):
    _b(_n, [128, 256], F32)
for _n in ("dep", "mm_", "yy", "ohb", "adat", "oc"):
    _b(_n, [128, 256], BF)
_b("tr", [128, 512], F32)
_b("kint", [128, 64], I32)
_b("yl", [128, 16], U16)
_b("pm", [128, 512], F32)
_b("code", [128, 64], I32)
_b("ask", [128, 32], F32)
_b("kk", [128, 32], BF)
_b("ktb", [16, 256], BF)
_b("bia", [128, 16], F32)
_b("sint", [128, 32], I32)
_b("dd", [128, 3072], BF)
_b("dso", [128, 3072], BF)
_b("rs0", [128, 512], BF)
_b("rs1", [128, 1024], BF)
_b("px32", [128, 2048], BF)
_b("cb", [128, 64], BF)
for _t in range(VIS):
    _b("ct%d" % _t, [128, 64], BF)
_b("dfl", [128, 64], F32)
_b("ol", [128, 16], U16)
_b("dsum", [128, 2], F32)
_b("cint", [128, 2], I32)
for _n in ("ones", "eye", "neye", "blk", "blk1", "blk8k", "tri", "trim", "dm32", "wmat", "j1", "j2", "kt", "r2"):
    _b(_n, [128, 128], BF)
for _n in ("sx", "px", "r1", "rm"):
    _b(_n, [128, 2048], BF)
for _n in ("blkf", "blk512", "onesf", "dmask"):
    _b(_n, [128, 128], F32)
_b("exs", [16, 512], BF)
_b("exf", [16, 128], F32)
_b("eyef", [16, 16], F32)
_b("io1", [128, 128], I32)
_b("io2", [128, 128], I32)
_b("pcol", [128, 4], I32)
_b("cols", [128, 16], F32)
_b("wti", [128, 1], I32)
_b("wtf", [128, 1], F32)
_b("limi", [8, 2], I32)
_b("limf", [8, 2], F32)
_b("limd", [8, 8], F32)
_b("tht", [128, 16], F32)
_b("thb", [128, 2], F32)
_b("dcon", [128, 16], F32)
_b("iod", [128, 16], I32)
_b("whoi", [128, 256], I32)
_b("pari", [128, 256], I32)
_b("parlh", [128, 512], I32)
_b("parb", [128, 512], BF)
_b("ypf", [128, 256], F32)
_b("dlo", [8, 4096], BF, "dram")
_b("dhi", [8, 4096], BF, "dram")
for _n in ("pz0", "pz1", "pz2", "pz3", "pk0", "pk1", "pf0", "pf1"):
    _b(_n, [128, 512], F32, "psum")

for _n in ("who", "est", "wt", "lim", "par", "claim0", "claim1", "plo", "phi", "pwin", "yv0", "yv1", "ye0", "ye1", "yp"):
    SEMAPHORES.append("l_" + _n)
for _t in range(1, VIS):
    for _h in range(2):
        for _k in "yv":
            SEMAPHORES += ["a%s%d%d" % (_k, _t, _h), "o%s%d%d" % (_k, _t, _h)]

PACK = {}
SCRATCH = {}
_ROOM = {}
_KEEP = ("claimw", "parw", "whoi", "pari", "parb", "ypf", "wti", "limi", "hl", "zl", "vl", "h2l", "yl", "ol", "dd", "adat")
for _n, (_w, _sh, _d) in BUF.items():
    if _w == "sbuf" and _n not in _KEEP and _n[:2] not in ("yb", "vb", "yn", "vn") and _sh[0] == 128 and _sh[1] <= 512:
        PACK[_n] = ("pack_" + _d, _ROOM.get(_d, 0))
        _ROOM[_d] = _ROOM.get(_d, 0) + (_sh[1] + 15) // 16 * 16
    else:
        SCRATCH[_n] = BUF[_n]
for _d in _ROOM:
    SCRATCH["pack_" + _d] = ("sbuf", [128, _ROOM[_d]], _d)

_CACHE = {}
CY, PCY, GATH, SCAT = 0.00083 * 1.1, 0.00042 * 1.1, 1.5, 3.5
VOV, SOV, POV, LAT = 0.04, 0.04, 0.02, 0.12
SEED, EPS = 0, 0.0
ONV = ()
LEAD = {"x0": 2.7, "t1": 1.3, "t0": -0.4, "x1": 0.0, "n1": 1.3, "z0": -0.2, "m1": -0.6, "p0": 2.9, "w1": -1.1, "p1": -0.1, "w0": -3.1, "e1": -0.6, "n0": 0.6, "m0": 1.2, "z1": 0.4, "e0": -0.3}
BONUS = {}
ERRB = (("pf0", "pf1"), ("pf0", "pf1"))
XL = 64


def S(name, a, b, step=1, p=128):
    return (name, a, b, step, p)


def IND(name, a, b, off, c, d):
    return (name, a, b, off, c, d, "ind")


def ap(T, s):
    if s[0] in PACK:
        r, o = PACK[s[0]]
        return T[r][0:s[4], o + s[1]:o + s[2]] if s[3] == 1 else T[r][0:s[4], o + s[1]:o + s[2]:s[3]]
    if len(s) == 7:
        return T[s[0]][:, s[1]:s[2]].indirect(T[s[3]][:, s[4]:s[5]])
    t = T[s[0]]
    if s[3] == 1:
        return t[0:s[4], s[1]:s[2]]
    return t[0:s[4], s[1]:s[2]:s[3]]


def regs(s):
    if len(s) == 7:
        return [(s[0], s[1], s[2]), (s[3], s[4], s[5])]
    return [(s[0], s[1], s[2])]


def width(s):
    if len(s) == 7:
        return 16 * (s[5] - s[4])
    return (s[2] - s[1] + s[3] - 1) // s[3]


def half(*ss):
    return all(BUF[s[0]][2] in (BF, U16) for s in ss)


def build(nE):
    ops = []
    since = [100000]
    part = [""]

    def add(q, fns, R, W, cost, sem=None, val=0, send=None):
        rr = [r for s in R for r in regs(s)]
        ww = [(s[0], s[1], s[2]) for s in W]
        offs = [(s[3], s[4], s[5]) for s in W if len(s) == 7]
        ops.append({"q": q, "f": fns, "R": rr + offs, "W": ww, "c": cost, "sem": sem, "val": val, "send": send, "at": len(ops) - since[0], "part": part[0]})
        return len(ops) - 1

    def vcost(n, f=1.0):
        return max(64, n * f) * CY + VOV

    def tt(out, a, b, op):
        n = width(b)
        if len(a) == 7:
            f = GATH
        else:
            f = 1.0 if "psum" in (BUF[a[0]][0], BUF[b[0]][0]) else 2.0
        add("V", [lambda g, T: g.vector.tensor_tensor(out=ap(T, out), in0=ap(T, a), in1=ap(T, b), op=op)], [a, b], [out], vcost(n, f))

    def cp(out, a):
        f = SCAT if len(out) == 7 else GATH if len(a) == 7 else 0.5 if half(out, a) else 1.0
        add("V", [lambda g, T: g.vector.tensor_copy(out=ap(T, out), in_=ap(T, a))], [a], [out], vcost(width(a), f))

    def ts(out, a, s1, op0, s2=None, op1=None):
        R = [a] + [s for s in (s1, s2) if isinstance(s, tuple)]

        def f(g, T):
            x1 = ap(T, s1) if isinstance(s1, tuple) else s1
            x2 = ap(T, s2) if isinstance(s2, tuple) else s2
            if op1 is None:
                return g.vector.tensor_scalar(out=ap(T, out), in0=ap(T, a), scalar1=x1, scalar2=None, op0=op0)
            return g.vector.tensor_scalar(out=ap(T, out), in0=ap(T, a), scalar1=x1, scalar2=x2, op0=op0, op1=op1)
        add("V", [f], R, [out], vcost(width(a), 0.5 if half(out, a) else 1.0))

    def scan(out, d0, d1, init, op0, op1):
        add("V", [lambda g, T: g.vector.tensor_tensor_scan(out=ap(T, out), data0=ap(T, d0), data1=ap(T, d1), initial=init, op0=op0, op1=op1)],
            [d0, d1], [out], vcost(width(d1), 0.5 if half(out, d0, d1) else 1.0))

    def red(out, a, op, absv=False):
        if absv:
            fn = lambda g, T: g.vector.tensor_reduce(out=ap(T, out), in_=ap(T, a), axis=AxisListType.X, op=op, apply_absolute_value=True)
        else:
            fn = lambda g, T: g.vector.tensor_reduce(out=ap(T, out), in_=ap(T, a), axis=AxisListType.X, op=op)
        add("V", [fn], [a], [out], vcost(width(a)))

    def fill(out, c):
        add("V", [lambda g, T: g.vector.memset(ap(T, out), c)], [], [out], vcost(width(out)))

    def act(out, a, func, bias=None, scale=None):
        R = [a] + ([bias] if isinstance(bias, tuple) else [])

        def f(g, T):
            kw = {}
            if bias is not None:
                kw["bias"] = ap(T, bias) if isinstance(bias, tuple) else bias
            if scale is not None:
                kw["scale"] = scale
            return g.scalar.activation(out=ap(T, out), in_=ap(T, a), func=func, **kw)
        add("S", [f], R, [out], max(64, width(a) * (GATH if len(a) == 7 else 1.0)) * CY + SOV)

    def gather(tag, out, a):
        if tag in ONV:
            cp(out, a)
        else:
            act(out, a, AF.Copy)

    def mm(groups):
        fns = []
        c = POV
        for (o, l, r, st, sp) in groups:
            fns.append(lambda g, T, o=o, l=l, r=r, st=st, sp=sp: g.tensor.matmul(out=ap(T, o), lhsT=ap(T, l), rhs=ap(T, r), start=st, stop=sp))
            c += max(64, width(r)) * PCY * (4 if BUF[r[0]][2] == F32 else 1)
        add("P", fns, [r for (o, l, r2, st, sp) in groups for r in (l, r2)], [x[0] for x in groups], c)

    def one(out, l, r):
        mm([(out, l, r, True, True)])

    def dma(q, sem, pairs, R, W, cost):
        add(q, [lambda g, T, o=o, i=i: (g.sync if q == "Y" else g.scalar).dma_start(o(T), i(T)) for (o, i) in pairs], R, W, cost, sem=sem, val=16 * len(pairs))

    def iota(out, pattern, base, cm):
        kw = {"allow_small_or_imprecise_dtypes": True} if BUF[out[0]][2] in (BF, F32) else {}
        add("G", [lambda g, T: g.iota(ap(T, out), pattern, base, cm, **kw)], [], [out], 0.13 + 2 * width(out) * CY)

    def asel(out, a, pattern, op, base, cm):
        add("G", [lambda g, T: g.affine_select(ap(T, out), ap(T, a), pattern, op, 0.0, base, cm)], [a], [out], 0.17 + 2 * width(out) * CY)

    def full(name):
        sh = BUF[name][1]
        return S(name, 0, sh[1], 1, sh[0])

    dma("Y", "l_who", [(lambda T: T.whoi[:], lambda T: T.who[:])], [], [full("whoi")], 2.0)
    dma("Y", "l_est", [(lambda T: T.yb0[:], lambda T: T.est[:])], [], [full("yb0")], 2.0)
    dma("Y", "l_wt", [(lambda T: T.wti[:], lambda T: T.wt[:])], [], [full("wti")], 2.0)
    dma("S", "l_claim0", [(lambda T: T.claimw[:, 0:2048], lambda T: T.claim[:, 0:2048])], [], [S("claimw", 0, 2048)], 3.0)
    dma("S", "l_claim1", [(lambda T: T.claimw[:, 2048:4096], lambda T: T.claim[:, 2048:4096])], [], [S("claimw", 2048, 4096)], 4.0)
    dma("Y", "l_par", [(lambda T: T.pari[:], lambda T: T.par[:])], [], [full("pari")], 2.0)
    dma("Y", "l_lim", [(lambda T: T.limi[:], lambda T: T.lim[:])], [], [full("limi")], 2.0)
    fill(full("ones"), 1.0)
    asel(full("blk1"), full("ones"), [[-16, 8], [0, 16]], A.is_ge, 0, 1)
    asel(full("blk"), full("blk1"), [[16, 8], [0, 16]], A.is_ge, 15, -1)
    asel(full("eye"), full("ones"), [[-1, 128]], A.is_equal, 0, 1)
    iota(S("pcol", 0, 1), [[0, 1]], 0, 1)
    cp(full("vb0"), full("whoi"))
    cp(full("vl"), full("vb0"))
    ts(S("parlh", 0, 256), full("pari"), 255, A.bitwise_and)
    ts(S("parlh", 256, 512), full("pari"), 8, A.logical_shift_right)
    cp(full("parb"), full("parlh"))
    dma("Y", "l_plo", [(lambda T: T.dlo[:], lambda T: T.parb[:, 0:256])], [S("parb", 0, 256)], [S("dlo", 0, 4096, 1, 8)], 2.0)
    dma("Y", "l_phi", [(lambda T: T.dhi[:], lambda T: T.parb[:, 256:512])], [S("parb", 256, 512)], [S("dhi", 0, 4096, 1, 8)], 2.0)
    dma("Y", "l_pwin", [(lambda T, i=i: T.parw[i::16, 16:4112], lambda T, i=i: (T.dhi if i % 2 else T.dlo)[:]) for i in range(16)],
        [S("dlo", 0, 4096, 1, 8), S("dhi", 0, 4096, 1, 8)], [S("parw", 16, 4112)], 8.0)
    cp(full("wtf"), full("wti"))
    ts(full("wmat"), full("blk"), S("wtf", 0, 1), A.mult)
    ts(S("pcol", 1, 2), S("pcol", 0, 1), 15, A.bitwise_and)
    ts(S("pcol", 2, 3), S("pcol", 0, 1), 1, A.bitwise_and)
    K16 = S("cols", 0, 1)
    CODE = S("cols", 1, 2)
    COLW = S("cols", 2, 3)
    COLA = S("cols", 3, 4)
    ACS = S("cols", 7, 8)
    ACB = S("cols", 8, 9)
    cp(K16, S("pcol", 1, 2))
    ts(CODE, K16, -1.0, A.mult, 16.0, A.add)
    ts(S("cols", 4, 5), K16, 1.0, A.is_equal, 256.0, A.mult)
    ts(S("cols", 5, 6), K16, 0.0, A.is_equal)
    tt(COLW, S("cols", 4, 5), S("cols", 5, 6), A.add)
    ts(COLA, K16, 16.0, A.mult)
    cp(S("cols", 6, 7), S("pcol", 2, 3))
    ts(ACS, S("cols", 6, 7), -255.0 / 256.0, A.mult, 1.0, A.add)
    ts(ACB, S("cols", 6, 7), -0.498, A.mult)
    fill(full("sx"), 0.0)
    for k in range(16):
        cp(S("sx", 129 * k, 128 * k + 128, 16), S("blk", 0, 128, 16))
    ts(full("px"), full("sx"), COLW, A.mult)
    ts(full("neye"), full("eye"), -1.0, A.mult)
    asel(full("tri"), full("blk"), [[1, 128]], A.is_gt, 0, -1)
    ts(full("trim"), full("eye"), -32.0, A.mult)
    tt(full("trim"), full("trim"), full("tri"), A.add)
    ts(full("dm32"), full("eye"), 32.0, A.mult)
    tt(full("dm32"), full("dm32"), full("blk"), A.subtract)
    asel(S("exs", 0, 128, 1, 16), S("ones", 0, 128, 1, 16), [[1, 128]], A.is_ge, 0, -16)
    asel(S("exs", 128, 256, 1, 16), S("exs", 0, 128, 1, 16), [[-1, 128]], A.is_ge, 15, 16)
    asel(S("exs", 256, 384, 1, 16), S("ones", 0, 128, 1, 16), [[1, 128]], A.is_ge, 128, -16)
    asel(S("exs", 384, 512, 1, 16), S("exs", 256, 384, 1, 16), [[-1, 128]], A.is_ge, -113, 16)
    cp(full("exf"), S("exs", 128, 256, 1, 16))
    cp(full("limf"), full("limi"))
    cp(full("onesf"), full("ones"))
    cp(full("eyef"), S("eye", 0, 16, 1, 16))
    ts(full("limd"), S("eyef", 0, 8, 1, 8), S("limf", 1, 2, 1, 8), A.mult, 32.0, A.mult)
    mm([(S("pk1", 0, 2), S("exf", 0, 128, 1, 8), full("limf"), True, True),
        (S("pk1", 8, 16), S("onesf", 0, 128, 1, 8), full("limd"), True, True)])
    cp(full("thb"), S("pk1", 0, 2))
    cp(S("thc0", 0, 1), S("pk1", 0, 1))
    fill(S("tht", 0, 8), -1.0)
    cp(S("tht", 8, 16), S("pk1", 8, 16))
    cp(full("blkf"), full("blk"))
    fill(full("r1"), 1.0)
    ts(S("r1", 0, 2048, 16), S("r1", 0, 2048, 16), 0.0, A.mult)
    fill(full("rm"), 0.0)
    ts(S("rm", 0, 2048, 16), S("rm", 0, 2048, 16), 256.0, A.add)
    QB = (BLOCKS[0][1] - BLOCKS[0][0]) // 16
    iota(S("io1", 0, 16 * QB), [[0, 16], [256, QB]], 0, 0)
    ts(S("j1", 0, 16 * QB), S("io1", 0, 16 * QB), COLA, A.add)
    iota(S("j2", 0, 16 * QB), [[1, 16], [0, QB]], 0, 0)
    iota(full("kt"), [[0, 8], [-1, 16]], 16, 0)
    iota(full("oc"), [[1, 256]], 0, 0)
    fill(full("r2"), 1.0)
    ts(S("r2", 1, 128, 16), S("r2", 1, 128, 16), 0.0, A.mult)
    iota(full("io2"), [[1, 128]], 128, -1)
    ts(full("io2"), full("io2"), 15, A.bitwise_and)
    ts(full("dmask"), full("io2"), 0.0, A.is_equal)
    ts(full("blk512"), full("blk"), 512.0, A.mult)
    ts(full("blk8k"), full("blk"), 8192.0, A.mult)
    iota(full("iod"), [[16, 16]], 4112, 0)
    ts(full("dcon"), full("iod"), K16, A.add)
    ts(full("px32"), full("px"), 32.0, A.mult)
    fill(full("cb"), -131072.0)
    for t in range(VIS):
        fill(full("ct%d" % t), float(2464 * t))
    fill(full("dd"), 4194304.0)
    for h in range(2):
        n, w = 512 + 512 * h, 128 + 128 * h
        fill(full("rs%d" % h), 0.0)
        ts(S("rs%d" % h, 0, n, w), S("rs%d" % h, 0, n, w), 4194304.0, A.add)
    turn = [0]

    def bank(names):
        turn[0] += 1
        return names[turn[0] % 2]

    def send(what, t, h):
        c = (128 * h, 128 * h + 128)
        key = "%s%d%d" % (what, t + 1, h)
        i = add("G", None, [S("%sn%d" % (what, t), *c)], [], 1.0, sem="o" + key, val=nE, send=(what, t + 1, h))
        add("N", None, [], [S("%sb%d" % (what, t + 1), *c)], 2.0, sem="a" + key, val=nE, send=i)

    def st_names(t, h):
        c = (128 * h, 128 * h + 128)
        v = S("vb%d" % t, *c)
        if t > 0:
            cp(S("vl", *c), v)
        act(S("q1", *c), v, AF.Identity, float(2464 * t - 131072), 32.0)

    def st_hash(t, h):
        c = (128 * h, 128 * h + 128)
        um, hi = S("um%d" % (t % 2), *c), S("hi%d" % (t % 2), *c)
        U, W = S("pz%d" % (2 * h), 256, 384), S("pz%d" % (2 * h), 384, 512)
        one(U, full("wmat"), S("yb%d" % t, *c))
        cp(S("t1", *c), U)
        ts(um, S("t1", *c), 4095, A.bitwise_and)
        tt(W, S("vb%d" % t, *c), um, A.mult)
        tt(S("t2", *c), W, S("q1", *c), A.add)
        ts(hi, S("t2", *c), 5, A.arith_shift_right, 4095, A.bitwise_and)
        cp(S("hl", *c), hi)

    def st_xgather(t, h):
        c = (128 * h, 128 * h + 128)
        for a in range(c[0], c[1], XL):
            gather("x%d" % (a // XL), S("x%d" % (t % 2), 16 * a, 16 * (a + XL)), IND("claimw", 0, 4096, "hl", a, a + XL))

    def st_pgather(t, n):
        c = BLOCKS[n]
        gather("p%d" % n, S("pr", 16 * c[0], 16 * c[1]), IND("parw", 16, 4112, "vl", *c))

    def st_z(t, n):
        c = BLOCKS[n]
        L = c[1] - c[0]
        X, X2 = 16 * c[0], 16 * c[1]
        b = "pz%d" % n
        p, w2, w3, q = [S(b, 64 * e, 64 * e + L) for e in range(4)]
        w4 = q
        um, hi, dep = S("um%d" % (t % 2), *c), S("hi%d" % (t % 2), *c), S("dep", *c)
        mm([(p, S("px", 128 * k, 128 * k + 128), S("pr", X + k, X2, 16), k == 0, k == 15) for k in range(16)])
        mm([(q, full("eye"), full("cb"), True, False), (q, full("eye"), full("ct%d" % t), False, False)] +
           [(q, S("px32", 128 * k, 128 * k + 128), S("pr", X + k, X2, 16), False, k == 15) for k in range(16)])
        tt(S("q2", *c), p, um, A.mult)
        tt(S("t3", *c), q, S("q2", *c), A.add)
        ts(S("t3", *c), S("t3", *c), 5, A.arith_shift_right, 4095, A.bitwise_and)
        cp(S("zl", *c), S("t3", *c))
        tt(S("dif", *c), p, S("vb%d" % t, *c), A.subtract)
        tt(S("d", X, X2), IND("claimw", 0, 4096, "zl", *c), S("x%d" % (t % 2), X, X2), A.subtract)
        act(S("ad", X, X2), S("d", X, X2), AF.Abs)
        mm([(w2, S("sx", 128 * k, 128 * k + 128), S("ad", X + k, X2, 16), k == 0, k == 15) for k in range(16)])
        ts(dep, w2, S("thc%d" % t, 0, 1), A.is_lt)
        mm([(w2, full("trim"), dep, True, True), (w3, full("dm32"), dep, True, True)])
        ts(w2, w2, K16, A.is_equal)
        tt(S("fh", *c), w2, hi, A.mult)
        ts(w3, w3, 17.0, A.is_ge)
        one(w2, full("blkf"), S("fh", *c))
        tt(S("dlt", *c), w2, hi, A.subtract)
        tt(w4, w3, S("dlt", *c), A.mult)
        tt(S("h2f", *c), w4, hi, A.add)
        cp(S("h2l", *c), S("h2f", *c))
        gather("s%d" % n, S("xs", X, X2), IND("claimw", 0, 4096, "h2l", *c))

    def st_m(t, n):
        c = BLOCKS[n]
        X, X2 = 16 * c[0], 16 * c[1]
        xs = S("xs", X, X2)
        scan(S("mx", X, X2), S("r1", 0, X2 - X), xs, 0.0, A.mult, A.max)
        scan(S("mn", X, X2), S("rm", 0, X2 - X), xs, 256.0, A.max, A.min)
        w = S("pz%d" % n, 64, 64 + c[1] - c[0])
        mm([(w, full("eye"), S("mx", X + 15, X2, 16), True, False), (w, full("eye"), S("mn", X + 15, X2, 16), False, True)])
        ts(S("mhalf", *c), w, 0.5, A.mult, -0.25, A.add)
        cp(S("mm_", *c), S("mhalf", *c))

    def st_newnames(t, h):
        c = (128 * h, 128 * h + 128)
        tt(S("vm", *c), S("dif", *c), S("dep", *c), A.mult)
        tt(S("vn%d" % t, *c), S("vm", *c), S("vb%d" % t, *c), A.add)
        if t < VIS - 1:
            send("v", t, h)
            red(S("dsum", h, h + 1), S("dep", *c), A.add)

    def st_count(t):
        if t == VIS - 1:
            return
        mm([(S("pk0", 0, 1), full("onesf"), S("dsum", 0, 1), True, False), (S("pk0", 0, 1), full("onesf"), S("dsum", 1, 2), False, True)])
        cp(S("cint", 0, 1), S("pk0", 0, 1))
        ts(S("cint", 1, 2), S("cint", 0, 1), 31, A.bitwise_and)
        tt(S("thc%d" % (t + 1), 0, 1), S("cint", 1, 2), S("thb", 0, 1), A.add)

    def distances(src, X, mid, out, scale, banks):
        L = width(mid)
        K = 512 // L
        for q in range(16 // K):
            b = bank(banks)
            gr = []
            for e in range(K):
                k = K * q + e
                o = S(b, L * e, L * e + L)
                gr += [(o, full("eye"), S(src, X + k, X + 16 * L, 16), True, False), (o, full("neye"), mid, False, True)]
            mm(gr)
            act(S(out, X + 512 * q, X + 512 * q + 512), S(b, 0, 512), AF.Abs, None, scale)

    def st_truth(t, n):
        c = BLOCKS[n]
        L = c[1] - c[0]
        X, X2, Q, h = 16 * c[0], 16 * c[1], L // 16, c[0] // 128
        distances("xs", X, S("mm_", *c), "af", 4096.0, ("pf0", "pf1"))
        bk, K = "pk%d" % h, c[0] % 128
        key = S(bk, K, K + L)
        mm([(key, full("eye"), S("j1", 0, L), True, False), (key, full("eye"), S("j2", 0, L), False, False)] +
           [(key, S("sx", 128 * a, 128 * a + 128), S("af", X + a, X2, 16), False, a == 15) for a in range(16)])
        B = 2 * c[0]
        cp(S("tr", B, B + L // 2), S(bk, K + L // 2, K + L))
        tt(S("tr", B + L // 2, B + L), S(bk, K, K + L // 2), S("tr", B, B + L // 2), A.min)
        a, w = B + L // 2, L // 4
        while w > Q:
            tt(S("tr", a + 2 * w, a + 3 * w), S("tr", a, a + w), S("tr", a + w, a + 2 * w), A.min)
            a, w = a + 2 * w, w // 2
        I = c[0] // 4
        tt(S("kint", I, I + Q), S("tr", a, a + w), S("tr", a + w, a + 2 * w), A.min)
        ts(S("kint", I + Q, I + 2 * Q), S("kint", I, I + Q), 4095, A.bitwise_and)
        cp(S("yl", c[0] // 16, c[1] // 16), S("kint", I + Q, I + 2 * Q))
        cp(S("yy", *c), IND("xs", X, X2, "yl", c[0] // 16, c[1] // 16))

    def st_est(t, h):
        c = (128 * h, 128 * h + 128)
        key = S("pk%d" % h, 384, 512)
        mm([(key, full("eye"), S("yy", *c), True, False), (key, full("eye"), S("yb%d" % t, *c), False, True)])
        ts(S("yhalf", *c), key, 0.5, A.mult, -0.25, A.add)
        cp(S("yn%d" % t, *c), S("yhalf", *c))
        if t < VIS - 1:
            send("y", t, h)

    def st_err(t, h):
        c = (128 * h, 128 * h + 128)
        X = 2048 * h
        distances("x%d" % (t % 2), X, S("yy", *c), "ae", 32.0, ERRB[h])
        bk, ba, E = "pk%d" % h, "pz%d" % (2 * h + 1), 256
        ek = S(bk, E, E + 128)
        mm([(ek, full("eye"), full("kt"), True, False)] +
           [(S(bk, E + k, E + 128, 16), S("ae", X + 128 * k, X + 128 * k + 128), S("blk", 0, 128, 16), False, k == 15) for k in range(16)])
        B = 256 * h
        scan(S("pm", B, B + 128), S("r1", 0, 128), ek, 0.0, A.mult, A.max)
        tt(S("tt_", 128 * h + 1, 128 * h + 128), S(bk, E + 1, E + 128), S("pm", B, B + 127), A.min)
        scan(S("pm", B + 129, B + 256), S("r2", 1, 128), S("tt_", 128 * h + 1, 128 * h + 128), 0.0, A.mult, A.max)
        m = S("pm", B + 15, B + 256, 16)
        cp(S("code", 32 * h, 32 * h + 16), m)
        tt(S("ask", 16 * h, 16 * h + 16), m, full("tht"), A.is_ge)
        ts(S("code", 32 * h + 16, 32 * h + 32), S("code", 32 * h, 32 * h + 16), 31, A.bitwise_and)
        tt(S("kk", 16 * h, 16 * h + 16), S("code", 32 * h + 16, 32 * h + 32), S("ask", 16 * h, 16 * h + 16), A.mult)
        one(S(ba, 0, 128, 1, 16), S("kk", 16 * h, 16 * h + 16), full("eye"))
        kt = S("ktb", 128 * h, 128 * h + 128, 1, 16)
        act(kt, S(ba, 0, 128, 1, 16), AF.Copy)
        RA, RB, C, N = S(ba, 128, 256), S(ba, 256, 384), S(ba, 384, 512), S(ba, 0, 128)
        mm([(RB, S("exs", 384, 512, 1, 16), kt, True, True), (RA, S("exs", 128, 256, 1, 16), kt, True, True)])
        v = S("vb%d" % t, *c)
        ts(S("ohb", *c), RB, CODE, A.is_equal)
        tt(S("sb", *c), S("ohb", *c), v, A.mult)
        mm([(C, full("blk512"), S("sb", *c), True, False), (C, full("blk8k"), S("ohb", *c), False, False), (C, full("eye"), S("oc", *c), False, True)])
        act(S("cr", *c), C, AF.Copy)
        tt(S("dg", *c), C, full("dmask"), A.mult)
        scan(S("cs", *c), S("r1", 0, 128), S("dg", *c), 0.0, A.mult, A.add)
        lst = S("cs", 128 * h + 15, 128 * h + 128, 16)
        ts(S("bia", 8 * h, 8 * h + 8), lst, -1.0, A.mult, 128.0, A.add)
        D0, DW = 1024 * h, 128 + 128 * h
        for b in range(8 * h, 8 * h + 8):
            w = 16 * b + 16
            at = D0 + DW * (b - 8 * h)
            act(S("dd", at, at + w), S("cr", 0, w), AF.Abs, S("bia", b, b + 1), 1.0)
            if b % 4 == 3:
                at += DW - 4 * DW
                scan(S("dso", at, at + 4 * DW), full("rs%d" % h), S("dd", at, at + 4 * DW), 0.0, A.max, A.min)
        ts(RA, RA, CODE, A.is_equal)
        tt(S("sa", *c), RA, v, A.mult)
        one(N, full("blkf"), S("sa", *c))
        ts(S("aint", *c), N, ACS, A.mult, ACB, A.add)
        ts(S("aint", *c), S("aint", *c), 255, A.bitwise_and)
        cp(S("adat", *c), S("aint", *c))
        cp(S("sint", 16 * h, 16 * h + 8), lst)
        ts(S("sint", 16 * h + 8, 16 * h + 16), S("sint", 16 * h, 16 * h + 8), 9, A.logical_shift_right)
        ts(S("dfl", 32 * h, 32 * h + 8), S("dso", D0 + DW - 1, D0 + 8 * DW, DW), 128.0, A.is_lt)
        tt(S("dfl", 32 * h + 8, 32 * h + 16), S("dfl", 32 * h, 32 * h + 8), S("dcon", 8 * h, 8 * h + 8), A.mult)
        tt(S("dfl", 32 * h + 16, 32 * h + 24), S("sint", 16 * h + 8, 16 * h + 16), S("dfl", 32 * h + 8, 32 * h + 16), A.max)
        cp(S("ol", 8 * h, 8 * h + 8), S("dfl", 32 * h + 16, 32 * h + 24))

    def st_scatter(t, h):
        c = (128 * h, 128 * h + 128)
        cp(IND("parw", 0, 4368, "ol", 8 * h, 8 * h + 8), S("adat", *c))

    nb = len(BLOCKS)
    for t in range(VIS):
        since[0] = len(ops)
        for h in range(2):
            part[0] = "x%d" % h
            st_names(t, h)
        for h in range(2):
            part[0] = "x%d" % h
            st_hash(t, h)
            st_xgather(t, h)
        for n in range(nb):
            part[0] = "p%d" % (2 * n // nb)
            st_pgather(t, n)
        for h in range(2):
            for n in range(h * nb // 2, (h + 1) * nb // 2):
                part[0] = "z%d" % h
                st_z(t, n)
                part[0] = "m%d" % h
                st_m(t, n)
            part[0] = "n%d" % h
            st_newnames(t, h)
        st_count(t)
        for h in range(2):
            part[0] = "t%d" % h
            for n in range(h * nb // 2, (h + 1) * nb // 2):
                st_truth(t, n)
            st_est(t, h)
        for h in range(2):
            part[0] = "e%d" % h
            st_err(t, h)
        for h in range(2):
            part[0] = "w%d" % h
            st_scatter(t, h)
    for h in range(2):
        c = (128 * h, 128 * h + 128)
        dma("Y", "l_yv%d" % h, [(lambda T, c=c: T.yv[:, c[0]:c[1]], lambda T, c=c: T.vn4[:, c[0]:c[1]])], [S("vn4", *c)], [], 2.0)
        dma("Y", "l_ye%d" % h, [(lambda T, c=c: T.ye[:, c[0]:c[1]], lambda T, c=c: T.yn4[:, c[0]:c[1]])], [S("yn4", *c)], [], 2.0)
    mm([(S("pf0", 0, 256), S("px", 128 * k, 128 * k + 128), S("parw", 16 + 256 * k, 272 + 256 * k), k == 0, k == 15) for k in range(16)])
    cp(full("ypf"), S("pf0", 0, 256))
    dma("Y", "l_yp", [(lambda T: T.yp[:], lambda T: T.ypf[:])], [full("ypf")], [], 2.0)

    hist = {}
    for i, o in enumerate(ops):
        dep = set()
        for (n, a, b) in o["R"]:
            ps = BUF[n][0] == "psum"
            for (j, a2, b2, w) in hist.get(n, ()):
                if (w and a < b2 and a2 < b) or (ps and ops[j]["q"] != o["q"]):
                    dep.add(j)
        for (n, a, b) in o["W"]:
            ps = BUF[n][0] == "psum"
            for (j, a2, b2, w) in hist.get(n, ()):
                if (a < b2 and a2 < b) or (ps and ops[j]["q"] != o["q"]):
                    dep.add(j)
        for (n, a, b) in o["R"]:
            hist.setdefault(n, []).append((i, a, b, False))
        for (n, a, b) in o["W"]:
            l = hist.setdefault(n, [])
            l[:] = [e for e in l if not (a <= e[1] and e[2] <= b) or BUF[n][0] == "psum"]
            l.append((i, a, b, True))
        if o["q"] == "N":
            dep = {o["send"]}
        dep.discard(i)
        o["D"] = dep
    return ops


def schedule(ops, seed=0, eps=0.0):
    n = len(ops)
    succ = [[] for _ in range(n)]
    for i, o in enumerate(ops):
        for j in o["D"]:
            succ[j].append(i)
    prio = [0.0] * n
    rnd = np.random.default_rng(seed).random(n)
    for i in range(n - 1, -1, -1):
        prio[i] = ops[i]["c"] + max([prio[j] + LAT for j in succ[i]], default=0.0)
    key = [(-(prio[i] + BONUS.get(ops[i]["at"], 0.0) + LEAD.get(ops[i]["part"], 0.0) + eps * float(rnd[i])), i) for i in range(n)]
    left = [len(o["D"]) for o in ops]
    heap = sorted(key[i] for i in range(n) if left[i] == 0)
    busy = {}
    est, fin = [0.0] * n, [0.0] * n
    order = []
    while heap:
        i = heap.pop(0)[1]
        o = ops[i]
        t = est[i]
        if o["q"] != "N":
            occ = 0.15 if o["sem"] and o["q"] in "YS" else o["c"]
            b = busy.setdefault(o["q"], [])
            at = len(b)
            while at > 0 and b[at - 1][1] > t:
                at -= 1
            while at < len(b) and max(t, b[at - 1][1] if at else 0.0) + occ > b[at][0]:
                at += 1
            t = max(t, b[at - 1][1] if at else 0.0)
            b.insert(at, (t, t + occ))
        o["start"] = t
        fin[i] = t + o["c"]
        order.append((t, len(order), i))
        for j in succ[i]:
            est[j] = max(est[j], fin[i] + LAT)
            left[j] -= 1
            if left[j] == 0:
                lo, hi = 0, len(heap)
                while lo < hi:
                    mid = (lo + hi) // 2
                    if heap[mid] < key[j]:
                        lo = mid + 1
                    else:
                        hi = mid
                heap.insert(lo, key[j])
    order.sort()
    return [i for _, _, i in order], max(fin)


SEMQ = {"V": "vv", "S": "ss", "P": "pp", "G": "gg"}


def plan(nE):
    if nE in _CACHE:
        return _CACHE[nE]
    ops = build(nE)
    order, total = schedule(ops, SEED, EPS)
    count = {s: 0 for s in SEMQ.values()}
    know, kq, out = {}, {}, []
    for i in order:
        o = ops[i]
        q = o["q"]
        mine = kq.setdefault(q, {})
        waits = {}
        if q != "N":
            for j in sorted(o["D"], key=lambda j: -ops[j]["start"]):
                s, v = ops[j]["ev"]
                if mine.get(s, 0) >= v:
                    continue
                waits[s] = max(waits.get(s, 0), v)
                for s2, v2 in know[j].items():
                    mine[s2] = max(mine.get(s2, 0), v2)
                mine[s] = max(mine.get(s, 0), v)
        know[i] = dict(mine) if q != "N" else {}
        if o["sem"]:
            o["ev"] = (o["sem"], o["val"])
        else:
            s = SEMQ[q]
            count[s] += len(o["f"])
            o["ev"] = (s, count[s])
        out.append((o, sorted(waits.items())))
    ends = {}
    for o in ops:
        s, v = o["ev"]
        ends[s] = max(ends.get(s, 0), v)
    _CACHE[nE] = (out, ends, total)
    return _CACHE[nE]


def rank_program(g, core, T, topo):
    rank = T.rank_of(core)
    if rank is None:
        return
    nxt = T.cores[(rank + 1) % len(T.cores)]
    eng = topo.engines(core, nxt)[::2]
    mask = 0
    for e in eng:
        mask |= 1 << e
    rid, pid, _ = topo.addr(nxt)
    steps, ends, _ = plan(len(eng))
    queue = {"V": g.vector, "S": g.scalar, "P": g.tensor, "G": g, "Y": g.sync}
    for o, waits in steps:
        q = o["q"]
        if q == "N":
            continue
        for s, v in waits:
            queue[q].wait_ge(T.sem[s], v)
        if o["send"]:
            k, t, h = o["send"]
            c = slice(128 * h, 128 * h + 128)
            g.remote_dma(out_ap=T["%sb%d" % (k, t)][:, c], in_ap=T["%sn%d" % (k, t - 1)][:, c], remote_sem=T.sem["a%s%d%d" % (k, t, h)],
                         local_sem=T.sem["o%s%d%d" % (k, t, h)], pid=pid, routing_id=rid, dma_engine_mask=mask)
        elif o["sem"]:
            for f in o["f"]:
                f(g, T).then_inc(T.sem[o["sem"]], 16)
        else:
            for f in o["f"]:
                f(g, T).then_inc(T.sem[SEMQ[q]], 1)
    for s, v in sorted(ends.items()):
        g.wait_ge(T.sem[s], v)
